import numpy as np, ml_dtypes
CORES = [40,41,42,43,44,45,46,47]
N = 8
BF = ml_dtypes.bfloat16
M, Q, CAP, V = 2048, 256, 96, 15
R = 2 ** 20; H = R - 2 ** 13
def shave(lo, hi, u, k):
    return [lo[i] + int((hi[i] - lo[i]) * k * u[3 + i]) for i in range(3)] + [hi[i] - int((hi[i] - lo[i]) * k * u[6 + i]) for i in range(3)]
def scene(rng, h, deep, uneven):
    U = rng.random((M, 12)).tolist(); u = U[0]; side = [int(h * (1 + 0.5 * u[i])) for i in range(3)]
    lo = [int(u[3 + i] * (2 * h - side[i])) - h for i in range(3)]; hi = [lo[i] + side[i] for i in range(3)]
    box = [lo + hi] * M; skip = [M] * M; todo = [(1, M, lo, hi, M, V - 1)]
    while todo:
        a, b, lo, hi, out, v = todo.pop(); u = U[a]; s = b - a
        if s <= 4 or (s <= v and (deep or u[0] < 0.3)):
            for n in range(a, b):
                w = U[n]; box[n] = shave(lo, hi, w, 0.25)
                k = n + 1 if deep or w[2] < 0.5 else n + 1 + int(w[11] * (b - n)); skip[n] = k if k < b else out
            if out > b:
                i = int(u[1] * 3); box[b - 1][3 + i] = box[b - 1][i] - 1
            continue
        c = 5 * 2 ** (v - 5) - 1; x = max(2, s - 1 - c); z = min(s - 3, c)
        m = a + 1 + (V - 2 if deep and a == 1 else x + int(u[9] * (z - x + 1)))
        i = int(u[1] * 3); cut = lo[i] + int((hi[i] - lo[i]) * (0.25 + 0.5 * u[10]))
        l2 = lo[:]; l2[i] = min(cut + 1, hi[i]); h2 = hi[:]; h2[i] = cut
        yes, no = ((lo, h2), (l2, hi)) if u[2] < 0.5 else ((l2, hi), (lo, h2))
        box[a] = shave(yes[0], yes[1], u, 0.125); skip[a] = m
        todo += [(a + 1, m) + yes + (out, v - 1), (m, b) + no + (out, v - 1)]
    w = 2 ** rng.integers(0, 17, M) if uneven else rng.integers(1, 2 ** 16 + 1, M)
    return np.concatenate([np.array(box, np.int64).T, np.array([skip], np.int64), (w * (2 * rng.integers(0, 2, M) - 1))[None]])
def scenes(rng, h, deep=False, uneven=False):
    t = np.zeros((N, 8, 16, M), np.int64)
    for r in range(N):
        for g in range(8):
            t[r, g, :8] = scene(rng, int(h[g]), deep, uneven)
    return t
def points(rng, h):
    h = np.asarray(h, np.int64).reshape(1, 8, 1, 1); return rng.integers(-h, h + 1, (N, 8, 3, Q))
def inbox(t, p):
    return ((t[:, :3, :1] <= p) & (p <= t[:, 3:6, :1])).all(-2)
def far(rng, n):
    return rng.integers(R - 2 ** 12, R + 1, (3, n))
def made(rng, t, p, s=0):
    for r in range(N):
        for q in [(r + s + i) % N for i in range(N)]:
            if q == r: continue
            k = inbox(t[q], p[r])
            for g in range(8):
                i = rng.permutation(np.flatnonzero(k[g]))[CAP:]
                if len(i): p[r, g][:, i] = far(rng, len(i))
    return {"nodes": t.reshape(N, 128, M).astype(np.int32), "pts": p.reshape(N, 24, Q).astype(np.int32)}
def setup_inputs(rng):
    return made(rng, scenes(rng, [H] * 8), points(rng, [H] * 8))
def setup_inputs_faces(rng):
    t = scenes(rng, [H] * 8); p = np.zeros((N, 8, 3, Q), np.int64)
    for g in range(8):
        q = rng.integers(0, N, (N, 1, Q)); n = rng.integers(0, M, (N, 1, Q)) * (rng.random((N, 1, Q)) > 0.25)
        p[:, g] = t[q, g, np.arange(3)[:, None] + 3 * rng.integers(0, 2, (N, 3, Q)), n] + rng.integers(-1, 2, (N, 3, Q))
    return made(rng, t, p)
def setup_inputs_full(rng):
    t = scenes(rng, [H] * 8); p = points(rng, [H] * 8); s = int(rng.integers(1, N))
    for r in range(N):
        b = t[(r + s) % N, :, :6, :1]; p[r] = b[:, :3] + np.floor(rng.random((8, 3, Q)) * (b[:, 3:] - b[:, :3] + 1)).astype(np.int64)
    return made(rng, t, p, s)
def setup_inputs_few(rng):
    t = scenes(rng, [H] * 8); p = points(rng, [H] * 8); o = rng.permutation(N); b, c = o[:2]; e = o[2:]; t[e, :, 3, 0] = t[e, :, 0, 0] - 1
    w = t[c, :, :6, :1]; p[c] = w[:, :3] + np.floor(rng.random((8, 3, Q)) * (w[:, 3:] - w[:, :3] + 1)).astype(np.int64)
    for g in range(8):
        p[b, g] = far(rng, Q); v = t[b, g, :3, 0] + np.floor(rng.random(3) * (t[b, g, 3:6, 0] - t[b, g, :3, 0] + 1)).astype(np.int64)
        p[b, g, :, :4] = v[:, None]; p[b, g, :, Q - 4:] = v[:, None]
    return made(rng, t, p)
def setup_inputs_deep(rng):
    return made(rng, scenes(rng, [H] * 8, deep=True), points(rng, [H] * 8))
def setup_inputs_spread(rng):
    h = 2 ** rng.integers(5, 20, 8); p = points(rng, h)
    return made(rng, scenes(rng, h, uneven=True), p >> (rng.integers(0, 6, (N, 8, 1, Q)) * (rng.random((N, 8, 1, Q)) < 0.25)))
def walk(t, p):
    nd = t.transpose(0, 2, 1); x = p.transpose(0, 1, 3, 2); c = np.zeros((N, 8, Q), np.int64); s = np.zeros_like(c); v = np.zeros_like(c)
    while (c < M).any():
        live = c < M; b = nd[np.arange(8)[:, None], np.minimum(c, M - 1)]
        hit = live & (b[..., :3] <= x).all(-1) & (x <= b[..., 3:6]).all(-1)
        s += hit * b[..., 7]; v += live; c = np.where(live, np.where(hit, c + 1, b[..., 6]), c)
    return s, v
def check_inputs(d):
    t = d["nodes"].astype(np.int64).reshape(N, 8, 16, M); p = d["pts"].astype(np.int64).reshape(N, 8, 3, Q); k = t[:, :, 6]; bad = []
    if (k <= np.arange(M)).any() or (k > M).any() or (k[:, :, 0] != M).any(): return ["skips"]
    if np.abs(t[:, :, :6]).max() > R or np.abs(p).max() > R: bad.append("coordinates")
    if np.abs(t[:, :, 7]).max() > 2 ** 16: bad.append("weights")
    if t[:, :, 8:].any(): bad.append("rows of zeros")
    n = np.stack([np.sum(inbox(t[q], p), axis=-1) for q in range(N)])
    n[np.arange(N), np.arange(N)] = 0
    if n.max() > CAP: bad.append("points in another rank's first box")
    if max(walk(t[q], p)[1].max() for q in range(N)) > V: bad.append("visits")
    return bad
def reference(nodes, pts):
    t = nodes.astype(np.int64).reshape(N, 8, 16, M); p = pts.astype(np.int64).reshape(N, 8, 3, Q); y = np.zeros((N, 8, Q), np.int64)
    for q in range(N):
        y += walk(t[q], p)[0]
    return {"y": y.astype(np.float32)}

@@ -1,0 +1,371 @@
+from concourse.bass import DstId, RemoteDMATransfer
+from concourse.mybir import AluOpType, ActivationFunctionType
+
+N = 8
+M = 2048
+MW = 2056
+STEPS = 14
+HALF = {"A": (0, 448), "B": (448, 480)}
+ALU = AluOpType
+COPY = ActivationFunctionType.Copy
+RELU = ActivationFunctionType.Relu
+
+SCRATCH = {}
+for _n, _w, _t in (
+        [(n, 1, "float32") for n in ("KF AF U2 V32 UV BASE PEN0 PEN1 TG0 TG1 R1 R2 R3 SG P16 VM V4 V1 W1 W2 W3").split()]
+        + [(n, 1, "int32") for n in "IK AI UI VI BI GI HI16".split()]
+        + [(n, 128, "int32") for n in "IR SKi Wi".split()]
+        + [(n, 128, "float32") for n in "CJ IRf IDf Wb MS ST Q1 GT".split()]
+        + [(n, 128, "bfloat16") for n in "TRI ONE AX0 SKh SKl Wh Wl HB NB".split()]
+        + [(n, 128, "float16") for n in "IDh L00 L01 L10 L11 SC SX GQ GX".split()]
+        + [("SO", 128, "uint16"), ("GO", 128, "uint16"), ("G8", 8, "float32"), ("CM", 8, "bfloat16"),
+           ("C1", 32, "bfloat16"), ("C2", 32, "bfloat16"), ("JT", 16, "float32"), ("N0", 8, "int32"),
+           ("BXi", 8, "int32"), ("BX", 8, "float32"), ("Pi", 256, "int32"), ("PL", 928, "float32"),
+           ("TW", MW, "float32"), ("AX", MW, "bfloat16"), ("F0", 2048, "bfloat16"), ("CP", 7 * 256, "float32"),
+           ("HIT", 512, "float16"), ("LOT", 512, "float16"), ("SM", 32, "float32"), ("SS", 32, "float32"),
+           ("SA", 192, "float32"), ("SB", 480, "float32"), ("Y0", 256, "float32"), ("Y1", 256, "float32"),
+           ("RW0", 288, "float32")]
+        + [("RW%d" % d, 128, "float32") for d in range(1, 8)]):
+    SCRATCH[_n] = ("sbuf", [128, _w], _t)
+for _h in "AB":
+    for _n, _w, _t in (("D1", 480, "bfloat16"), ("D2", 480, "bfloat16"), ("OF", 32, "uint16"), ("NX", 32, "float16"),
+                       ("TT", 32, "float32"), ("XT", 32, "float16"), ("WT", 32, "float32"), ("ZZ", 64, "float32")):
+        SCRATCH[_n + _h] = ("sbuf", [128, _w], _t)
+PSUM = ["PF", "PR", "PSA", "PSB", "EXA", "EXB", "ACA", "ACB"]
+for _n in PSUM:
+    SCRATCH[_n] = ("psum", [128, 512], "float32")
+
+DMASEMS = ["dN0", "dP", "dSW", "dT0", "dT1", "dAX", "dY"]
+SEMAPHORES = (["cV", "cA", "cP", "cG", "box", "ls"] + DMASEMS
+              + ["pt%d" % d for d in range(1, 8)] + ["rt%d" % d for d in range(1, 8)])
+
+
+def rank_program(g, core, T, topo):
+    rank = T.rank_of(core)
+    if rank is None:
+        return
+    cores = T.cores
+    queue = {"V": g.vector, "A": g.scalar, "P": g.tensor, "G": g, "S": g.sync}
+    total = {}
+    seen = {}
+    wr, rd = {}, {}
+
+    def await_(q, handles):
+        need = {}
+        for (_, sem, val) in handles:
+            if sem in DMASEMS:
+                val = total[sem]
+            need[sem] = max(need.get(sem, 0), val)
+        for sem in sorted(need):
+            if seen.get((q, sem), 0) < need[sem]:
+                queue[q].wait_ge(T.sem[sem], need[sem])
+                seen[(q, sem)] = need[sem]
+
+    def deps(q, reads, writes):
+        hs = []
+        for t in reads:
+            hs += wr.get(t, [])
+            if t in PSUM:
+                hs += [h for h in rd.get(t, []) if h[0] != q]
+        for t in writes:
+            hs += [h for h in wr.get(t, []) + rd.get(t, []) if h[0] != q]
+        await_(q, hs)
+
+    def note(h, reads, writes, add=False):
+        for t in reads:
+            rd.setdefault(t, []).append(h)
+        for t in writes:
+            if add:
+                wr.setdefault(t, []).append(h)
+            else:
+                wr[t] = [h]
+                rd[t] = []
+
+    def op(q, method, reads, writes, *args, add=False, **kw):
+        deps(q, reads, writes)
+        sem = "c" + q
+        total[sem] = total.get(sem, 0) + 1
+        h = (q, sem, total[sem])
+        method(*args, **kw).then_inc(T.sem[sem], 1)
+        note(h, reads, writes, add)
+
+    def dma(q, sem, out, in_, reads, writes, add=False):
+        deps(q, reads, writes)
+        total[sem] = total.get(sem, 0) + 16
+        queue[q].dma_start(out, in_).then_inc(T.sem[sem], 16)
+        note((None, sem, total[sem]), reads, writes, add)
+
+    def remote(out_ap, in_ap, dst, rsem, reads):
+        deps("G", reads, [])
+        rid, pid, _ = topo.addr(dst)
+        total["ls"] = total.get("ls", 0) + len(topo.engines(core, dst))
+        g.remote_dma(out_ap, in_ap, T.sem[rsem], T.sem.ls, pid, rid, topo.mask(core, dst))
+
+    v, a, p = g.vector, g.scalar, g.tensor
+
+    def ts(reads, writes, out, in0, s1, s2, *ops):
+        op("V", v.tensor_scalar, reads, writes, out, in0, s1, s2, *ops)
+
+    def tt(reads, writes, out, in0, in1, o):
+        op("V", v.tensor_tensor, reads, writes, out, in0, in1, o)
+
+    def vc(reads, writes, out, in_):
+        op("V", v.tensor_copy, reads, writes, out, in_)
+
+    def fill(tag, ap, c):
+        op("V", v.memset, [], [tag], ap, c)
+
+    def mm(reads, writes, out, lhsT, rhs, start, stop):
+        op("P", p.matmul, reads, writes, out, lhsT, rhs, start, stop)
+
+    def act(reads, writes, out, in_, func, **kw):
+        op("A", a.activation, reads, writes, out, in_, func, **kw)
+
+    dma("S", "dN0", T.N0[:], T.nodes[:, 0:8], [], ["N0"])
+    fill("Pi", T.Pi[:], 0)
+    op("G", g.iota, [], ["IK"], T.IK[:], [[1, 1]], 0, 1)
+    op("G", g.iota, [], ["IR"], T.IR[:], [[1, 128]], 0, 0)
+    for i in range(6):
+        dma("S" if i < 3 else "A", "dP", T.Pi[i::16, :], T.pts[i % 3::3, :], [], ["Pi"], add=True)
+    dma("S", "dSW", T.SKi[:], T.nodes[6::16, :], [], ["SKi"])
+    dma("A", "dSW", T.Wi[:], T.nodes[7::16, :], [], ["Wi"])
+    dsts = [cores[(rank + e) % N] for e in range(1, N)]
+    deps("G", ["N0"], [])
+    ids = []
+    for dcore in dsts:
+        rid, pid, _ = topo.addr(dcore)
+        ids.append(DstId(rid=rid, pnc=pid))
+    lanes = len(topo.engines(core, dsts[0]))
+    total["ls"] = lanes
+    g.remote_dma_fused([RemoteDMATransfer(
+        dst_ids=ids, dma_engine_mask=topo.mask(core, dsts[0]), remote_sem=T.sem.box, srcs=[T.N0[:, 0:1]],
+        dsts=[T.BXi[:, N - e:N - e + 1] for e in range(1, N)])], local_sem=T.sem.ls)
+    total["box"] = (N - 1) * lanes
+    note((None, "box", total["box"]), [], ["BXi"])
+    dma("G", "dT0", T.TW[:, 0:1024], T.nodes[:, 0:1024], [], ["TWa"])
+    dma("G", "dT1", T.TW[:, 1024:2048], T.nodes[:, 1024:2048], [], ["TWb"])
+    op("G", g.iota, [], ["CJ"], T.CJ[:], [[0, 8], [-128, 2], [0, 8]], 255, -1, allow_small_or_imprecise_dtypes=True)
+
+    vc(["IK"], ["KF"], T.KF[:], T.IK[:])
+    ts(["IK"], ["AI"], T.AI[:], T.IK[:], 15, None, ALU.bitwise_and)
+    vc(["IR"], ["IRf"], T.IRf[:], T.IR[:])
+    vc(["AI"], ["AF"], T.AF[:], T.AI[:])
+    ts(["IK"], ["UI"], T.UI[:], T.IK[:], 5, None, ALU.logical_shift_right)
+    ts(["IK"], ["VI"], T.VI[:], T.IK[:], 1, 3, ALU.logical_shift_right, ALU.bitwise_and)
+    ts(["IK"], ["BI"], T.BI[:], T.IK[:], 24, None, ALU.bitwise_and)
+    ts(["IK"], ["GI"], T.GI[:], T.IK[:], 1, None, ALU.bitwise_and)
+    ts(["IK"], ["HI16"], T.HI16[:], T.IK[:], 4, None, ALU.logical_shift_right)
+    ts(["AF"], ["R1"], T.R1[:], T.AF[:], 2.5, None, ALU.is_gt)
+    ts(["AF"], ["R2"], T.R2[:], T.AF[:], 5.5, -2.0, ALU.is_lt, ALU.mult)
+    ts(["AF"], ["VM"], T.VM[:], T.AF[:], 5.5, None, ALU.is_lt)
+    vc(["HI16"], ["P16"], T.P16[:], T.HI16[:])
+    tt(["R1", "R2"], ["R3"], T.R3[:], T.R1[:], T.R2[:], ALU.mult)
+    ts(["IRf", "P16"], ["G8"], T.G8[:], T.IRf[:, 0:8], T.P16[:, 0:1], None, ALU.is_equal)
+    ts(["R3"], ["SG"], T.SG[:], T.R3[:], 1.0, None, ALU.add)
+    ts(["G8", "VM"], ["CM"], T.CM[:], T.G8[:], T.VM[:, 0:1], None, ALU.mult)
+    ts(["Pi", "SG"], ["PL0"], T.PL[:, 0:256], T.Pi[:], T.SG[:, 0:1], None, ALU.mult)
+    fill("AXm", T.AX[:, 0:M], 65536.0)
+    fill("AXs", T.AX[:, M:MW], 1024.0)
+    fill("TWs", T.TW[:, M:MW], 4194304.0)
+    vc(["SKi"], ["SKh"], T.SKh[:], T.SKi[:])
+    ts(["Wi"], ["Wb"], T.Wb[:], T.Wi[:], 65536.0, None, ALU.add)
+    tt(["SKi", "SKh"], ["SKl"], T.SKl[:], T.SKi[:], T.SKh[:], ALU.subtract)
+    vc(["Wb"], ["Wh"], T.Wh[:], T.Wb[:])
+    tt(["Wb", "Wh"], ["Wl"], T.Wl[:], T.Wb[:], T.Wh[:], ALU.subtract)
+    wr["AX"] = []
+    for i, n in enumerate(("SKh", "SKl", "Wh", "Wl")):
+        dma("S", "dAX", T.AX[i::16, 0:M], T[n][:], [n, "AXm"], ["AX"], add=True)
+    wr["AX"] = wr["AX"] + wr["AXm"] + wr["AXs"]
+    ts(["UI"], ["U2"], T.U2[:], T.UI[:], 2.0, None, ALU.mult)
+    ts(["VI"], ["V32"], T.V32[:], T.VI[:], 32.0, None, ALU.mult)
+    ts(["GI"], ["PEN0"], T.PEN0[:], T.GI[:], 1000.0, None, ALU.mult)
+    ts(["GI"], ["PEN1"], T.PEN1[:], T.GI[:], -1000.0, 1000.0, ALU.mult, ALU.add)
+    tt(["U2", "V32"], ["UV"], T.UV[:], T.U2[:], T.V32[:], ALU.add)
+    tt(["UV", "BI"], ["BASE"], T.BASE[:], T.UV[:], T.BI[:], ALU.add)
+    tt(["BASE", "PEN0"], ["TG0"], T.TG0[:], T.BASE[:], T.PEN0[:], ALU.add)
+    tt(["BASE", "PEN1"], ["TG1"], T.TG1[:], T.BASE[:], T.PEN1[:], ALU.add)
+    for x in (0, 1):
+        for y in (0, 1):
+            n = "L%d%d" % (x, y)
+            ts(["IRf", "TG%d" % x], [n], T[n][:], T.IRf[:], float(-y), T["TG%d" % x][:, 0:1], ALU.add, ALU.is_equal)
+    ts(["IRf", "KF"], ["TRI"], T.TRI[:], T.IRf[:], T.KF[:, 0:1], None, ALU.is_gt)
+    fill("ONE", T.ONE[:], 1.0)
+    fill("C1", T.C1[:], 0.0)
+    fill("C2", T.C2[:], 0.0)
+    ts(["AF"], ["V4"], T.V4[:], T.AF[:], 4.0, None, ALU.is_equal)
+    ts(["AF"], ["V1"], T.V1[:], T.AF[:], 1.5, None, ALU.is_lt)
+    ts(["AF"], ["W1"], T.W1[:], T.AF[:], 1.5, None, ALU.is_gt)
+    ts(["AF"], ["W2"], T.W2[:], T.AF[:], 3.5, None, ALU.is_lt)
+    tt(["W1", "W2"], ["W3"], T.W3[:], T.W1[:], T.W2[:], ALU.mult)
+    await_("V", wr["C1"] + wr["C2"])
+    for (n, q, col, f) in (("C1", 0, "VM", 4096.0), ("C1", 1, "VM", -2048.0), ("C1", 3, "VM", -2048.0),
+                           ("C2", 0, "V4", 2.0 ** -16), ("C2", 1, "W3", 2.0 ** -6), ("C2", 2, "V1", 1.0),
+                           ("C2", 3, "V4", 2.0 ** -6)):
+        ts(["G8", col], [n], T[n][:, q::4], T.G8[:], T[col][:, 0:1], f, ALU.mult, ALU.mult)
+    for h in "AB":
+        fill("PS" + h, T["PS" + h][:, 0:128], 0.0)
+        fill("OF" + h, T["OF" + h][:], 1)
+        ts(["IRf"], ["NX" + h], T["NX" + h][:], T.IRf[:, 0:32], 0.0, 1.0, ALU.mult, ALU.add)
+    ts(["IRf", "KF"], ["IDf"], T.IDf[:], T.IRf[:], T.KF[:, 0:1], None, ALU.is_equal)
+    ts(["IRf", "KF"], ["IDh"], T.IDh[:], T.IRf[:], T.KF[:, 0:1], None, ALU.is_equal)
+    for b in range(4):
+        ts(["IRf"], ["HIT"], T.HIT[:, b * 128:b * 128 + 128], T.IRf[:], 0.0, None, ALU.mult)
+        ts(["IRf"], ["LOT"], T.LOT[:, b * 128:b * 128 + 128], T.IRf[:], 0.0, None, ALU.mult)
+    act(["TWa", "SG"], ["TWa"], T.TW[:, 0:1024], T.TW[:, 0:1024], COPY, scale=T.SG[:, 0:1])
+    act(["TWb", "SG"], ["TWb"], T.TW[:, 1024:M], T.TW[:, 1024:M], COPY, scale=T.SG[:, 0:1])
+    TW = ["TWa", "TWb", "TWs"]
+
+    ts(["N0", "SG"], ["BX0"], T.BX[:, 0:1], T.N0[:, 0:1], T.SG[:, 0:1], None, ALU.mult)
+    ts(["BXi", "SG"], ["BX1"], T.BX[:, 1:8], T.BXi[:, 1:8], T.SG[:, 0:1], None, ALU.mult)
+    for d in list(range(1, 8)) + [0]:
+        ts(["PL0", "BX%d" % min(d, 1)], ["F0_%d" % d], T.F0[:, d * 256:d * 256 + 256], T.PL[:, 0:256], T.BX[:, d:d + 1], None, ALU.is_lt)
+        for jb in (0, 1):
+            c = d * 16 + jb * 8
+            mm(["F0_%d" % d, "CM"], ["PF"], T.PF[:, c:c + 8], T.F0[:, d * 256 + jb * 128:d * 256 + jb * 128 + 128], T.CM[:], True, True)
+    ts(["PF"], ["HB"], T.HB[:], T.PF[:, 0:128], 0.5, None, ALU.is_lt)
+    ts(["PF"], ["NB"], T.NB[:], T.PF[:, 0:128], 0.5, None, ALU.is_gt)
+    tt(["NB", "CJ"], ["MS"], T.MS[:], T.NB[:], T.CJ[:], ALU.mult)
+    mm(["HB", "TRI"], ["PR"], T.PR[:, 0:128], T.TRI[:], T.HB[:], True, False)
+    for d in range(8):
+        mm(["HB", "ONE"], ["PR"], T.PR[:, d * 16 + 8:d * 16 + 16], T.ONE[:], T.HB[:, d * 16:d * 16 + 8], False, d == 7)
+
+    def exchange(x, out, blocks):
+        for b in range(blocks):
+            for g0 in (0, 1):
+                for p4 in (0, 1):
+                    n = "L%d%d" % (g0, p4)
+                    mm([x, n], [out], T[out][:, b * 32 + g0 * 16:b * 32 + g0 * 16 + 16], T[n][:],
+                       T[x][:, b * 32 + p4 * 16:b * 32 + p4 * 16 + 16], p4 == 0, p4 == 1)
+
+    tt(["PR", "MS"], ["SC"], T.SC[:], T.PR[:, 0:128], T.MS[:], ALU.add)
+    op("V", v.transpose, ["SC"], ["SX"], T.SX[:], T.SC[:])
+    exchange("SX", "EXA", 4)
+    for d in range(8):
+        fill("RZ%d" % d, T["RW%d" % d][:, (256 if d == 0 else 96):(288 if d == 0 else 128)], 0.0)
+    op("V", v.transpose, ["EXA"], ["ST"], T.ST[:], T.EXA[:, 0:128])
+    vc(["ST"], ["SO"], T.SO[:], T.ST[:])
+    for d in range(1, 8):
+        vc(["PL0", "SO"], ["CP%d" % d], T.CP[:, (d - 1) * 256:d * 256].indirect(T.SO[:, d * 16:d * 16 + 16]), T.PL[:, 0:256])
+        remote(T.PL[:, 256 + 96 * (d - 1):256 + 96 * d], T.CP[:, (d - 1) * 256:(d - 1) * 256 + 96],
+               cores[(rank + d) % N], "pt%d" % d, ["CP%d" % d] + ["RZ%d" % k for k in range(8)])
+        total["pt%d" % d] = len(topo.engines(cores[(rank - d) % N], core))
+        note((None, "pt%d" % d, total["pt%d" % d]), [], ["PL%d" % d])
+        if d == 1:
+            ts(["AX", "IRf"], ["AX0"], T.AX0[:], T.IRf[:], 0.0, T.AX[:, 0:1], ALU.mult, ALU.add)
+
+    def blocks(h):
+        n = HALF[h][1]
+        return [(b, b * 128, min(n, b * 128 + 128)) for b in range((n + 127) // 128)]
+
+    def part(h, k):
+        return (0, 256) if k == 0 else (256, HALF[h][1])
+
+    def sources(h, k):
+        if h == "A":
+            return ["PL0"] if k == 0 else ["PL1", "PL2"]
+        return ["PL3", "PL4", "PL5"] if k == 0 else ["PL5", "PL6", "PL7"]
+
+    def visit_v(h, k, t):
+        lo, hi = part(h, k)
+        base = HALF[h][0]
+        out, pt = T["D1" + h][:, lo:hi], T.PL[:, base + lo:base + hi]
+        rs, ws = TW + sources(h, k), ["D1%s%d" % (h, k)]
+        if t == 1:
+            ts(rs, ws, out, pt, T.TW[:, 1:2], None, ALU.is_lt)
+        else:
+            tt(rs + ["OF" + h], ws, out, T.TW[:].indirect(T["OF" + h][:, lo // 16:hi // 16]), pt, ALU.is_gt)
+
+    def visit_a(h, k):
+        lo, hi = part(h, k)
+        act(["AX", "OF" + h], ["D2%s%d" % (h, k)], T["D2" + h][:, lo:hi],
+            T.AX[:].indirect(T["OF" + h][:, lo // 16:hi // 16]), COPY)
+
+    def sums(h, k):
+        lo, hi = part(h, k)
+        for (b, x, y) in blocks(h):
+            if lo <= x < hi:
+                out = T["PS" + h][0:y - x, b * 32:b * 32 + 32]
+                mm(["D2%s%d" % (h, k), "C2"], ["PS" + h], out, T["D2" + h][:, x:y], T.C2[:], True, False)
+                mm(["D1%s%d" % (h, k), "C1"], ["PS" + h], out, T["D1" + h][:, x:y], T.C1[:], False, True)
+
+    def next_1(h):
+        ps = T["PS" + h]
+        tt(["PS" + h, "NX" + h], ["TT" + h], T["TT" + h][:], ps[:, 0:128:4], T["NX" + h][:], ALU.add)
+        tt(["PS" + h, "TT" + h], ["NX" + h], T["NX" + h][:], ps[:, 2:128:4], T["TT" + h][:], ALU.min)
+        op("V", v.transpose, ["NX" + h], ["XT" + h], T["XT" + h][:], T["NX" + h][:])
+
+    def next_2(h):
+        op("V", v.transpose, ["EX" + h], ["WT" + h], T["WT" + h][:], T["EX" + h][:, 0:32])
+        vc(["WT" + h], ["OF" + h], T["OF" + h][:], T["WT" + h][:])
+
+    def weigh(h):
+        act(["PS" + h], ["ZZ" + h], T["ZZ" + h][:], T["PS" + h][:, 1:128:2], RELU)
+
+    def add_up(h, t):
+        mm(["ZZ" + h, "IDf"], ["AC" + h], T["AC" + h][:, 0:64], T.IDf[:], T["ZZ" + h][:], t == 0, t == STEPS)
+
+    for h in "AB":
+        for (b, x, y) in blocks(h):
+            mm(["AX0", "C2"], ["PS" + h], T["PS" + h][0:y - x, b * 32:b * 32 + 32], T.AX0[:, 0:y - x], T.C2[:], True, True)
+        weigh(h)
+        add_up(h, 0)
+    for s in range(2 * STEPS):
+        t = s // 2 + 1
+        h, o = ("A", "B") if s % 2 == 0 else ("B", "A")
+        to = t if h == "B" else t - 1
+        visit_v(h, 0, t)
+        visit_a(h, 0)
+        if to >= 1:
+            if to < STEPS:
+                next_1(o)
+            weigh(o)
+        sums(h, 0)
+        if 1 <= to < STEPS:
+            exchange("XT" + o, "EX" + o, 1)
+        visit_v(h, 1, t)
+        visit_a(h, 1)
+        sums(h, 1)
+        if to >= 1:
+            if to < STEPS:
+                next_2(o)
+            add_up(o, to)
+    weigh("B")
+
+    def finish(h, tp):
+        ac = T["AC" + h]
+        vc(["AC" + h], ["SM"], T.SM[:], ac[:, 1:64:2])
+        tt(["AC" + h, "SM"], ["SS"], T.SS[:], ac[:, 0:64:2], T.SM[:], ALU.subtract)
+        vc(["SS"], ["HIT"], T.HIT[:, 0:512:16], T.SS[:])
+        tt(["SS", "HIT"], ["LOT"], T.LOT[:, 0:512:16], T.SS[:], T.HIT[:, 0:512:16], ALU.subtract)
+        for (b, x, y) in blocks(h):
+            mm(["HIT", "IDh"], [tp], T[tp][:, x:y], T.HIT[:, b * 128:b * 128 + 128], T.IDh[:, 0:y - x], True, False)
+            mm(["LOT", "IDh"], [tp], T[tp][:, x:y], T.LOT[:, b * 128:b * 128 + 128], T.IDh[:, 0:y - x], False, True)
+
+    finish("A", "PF")
+    act(["PF"], ["SA"], T.SA[:], T.PF[:, 256:448], COPY, scale=64.0)
+    act(["PF"], ["RV0"], T.RW0[:, 0:256], T.PF[:, 0:256], COPY, scale=64.0)
+    add_up("B", STEPS)
+    finish("B", "EXB")
+    act(["EXB"], ["SB"], T.SB[:], T.EXB[:, 0:480], COPY, scale=64.0)
+    for d in range(1, 8):
+        src = T.SA[:, 96 * (d - 1):96 * d] if d < 3 else T.SB[:, 96 * (d - 3):96 * (d - 2)]
+        remote(T["RW%d" % d][:, 0:96], src, cores[(rank - d) % N], "rt%d" % d, ["SA" if d < 3 else "SB"])
+        total["rt%d" % d] = len(topo.engines(cores[(rank + d) % N], core))
+        note((None, "rt%d" % d, total["rt%d" % d]), [], ["RV%d" % d])
+    ts(["PR"], ["Q1"], T.Q1[:], T.PR[:, 0:128], -96.0, None, ALU.add)
+    ts(["CJ"], ["JT"], T.JT[:], T.CJ[:, 0:16], -1.0, -1.0, ALU.mult, ALU.add)
+    tt(["Q1", "HB"], ["GQ"], T.GQ[:, 16:128], T.Q1[:, 16:128], T.HB[:, 16:128], ALU.mult)
+    op("V", v.tensor_tensor, ["JT", "HB"], ["GQ"], T.GQ[:, 0:16], T.JT[:], T.HB[:, 0:16], ALU.mult, add=True)
+    op("V", v.transpose, ["GQ"], ["GX"], T.GX[:], T.GQ[:])
+    exchange("GX", "EXA", 4)
+    op("V", v.transpose, ["EXA"], ["GT"], T.GT[:], T.EXA[:, 0:128])
+    ts(["GT"], ["GO0"], T.GO[:, 0:16], T.GT[:, 0:16], 256.0, None, ALU.add)
+    ts(["GT"], ["GO1"], T.GO[:, 16:128], T.GT[:, 16:128], 96.0, None, ALU.add)
+    vc(["RV0", "RZ0", "GO0"], ["Y0"], T.Y0[:], T.RW0[:].indirect(T.GO[:, 0:16]))
+    for d in range(1, 8):
+        x, y = ("Y0", "Y1") if d % 2 else ("Y1", "Y0")
+        tt([x, "RV%d" % d, "RZ%d" % d, "GO1"], [y], T[y][:], T["RW%d" % d][:].indirect(T.GO[:, d * 16:d * 16 + 16]), T[x][:], ALU.add)
+    dma("S", "dY", T.y[:, :], T.Y1[0::16, :], ["Y1"], ["y"])
+    for sem in sorted(total):
+        if max([seen.get((q, sem), 0) for q in queue]) < total[sem]:
+            g.wait_ge(T.sem[sem], total[sem])

@@ -5,7 +5,7 @@ N = 8
 M = 2048
 MW = 2056
 STEPS = 14
-HALF = {"A": (0, 448), "B": (448, 480)}
+BATCH = [(0, 320), (320, 320), (640, 288)]
 ALU = AluOpType
 COPY = ActivationFunctionType.Copy
 RELU = ActivationFunctionType.Relu
@@ -14,24 +14,24 @@ SCRATCH = {}
 for _n, _w, _t in (
         [(n, 1, "float32") for n in ("KF AF U2 V32 UV BASE PEN0 PEN1 TG0 TG1 R1 R2 R3 SG P16 VM V4 V1 W1 W2 W3").split()]
         + [(n, 1, "int32") for n in "IK AI UI VI BI GI HI16".split()]
-        + [(n, 128, "int32") for n in "IR SKi Wi".split()]
+        + [(n, 128, "int32") for n in "SKi Wi".split()]
         + [(n, 128, "float32") for n in "CJ IRf IDf Wb MS ST Q1 GT".split()]
         + [(n, 128, "bfloat16") for n in "TRI ONE AX0 SKh SKl Wh Wl HB NB".split()]
         + [(n, 128, "float16") for n in "IDh L00 L01 L10 L11 SC SX GQ GX".split()]
+        + [(n, 256, "float32") for n in "A0 A1 A2 Y0 Y1 Y2".split()]
         + [("SO", 128, "uint16"), ("GO", 128, "uint16"), ("G8", 8, "float32"), ("CM", 8, "bfloat16"),
            ("C1", 32, "bfloat16"), ("C2", 32, "bfloat16"), ("JT", 16, "float32"), ("N0", 8, "int32"),
            ("BXi", 8, "int32"), ("BX", 8, "float32"), ("Pi", 256, "int32"), ("PL", 928, "float32"),
            ("TW", MW, "float32"), ("AX", MW, "bfloat16"), ("F0", 2048, "bfloat16"), ("CP", 7 * 256, "float32"),
-           ("HIT", 512, "float16"), ("LOT", 512, "float16"), ("SM", 32, "float32"), ("SS", 32, "float32"),
-           ("SA", 192, "float32"), ("SB", 480, "float32"), ("Y0", 256, "float32"), ("Y1", 256, "float32"),
-           ("RW0", 288, "float32")]
+           ("HIT", 1152, "float16"), ("LOT", 1152, "float16"), ("SM", 72, "float32"), ("SS", 72, "float32"),
+           ("SA", 672, "float32"), ("ZZ", 144, "float32"), ("RW0", 288, "float32")]
         + [("RW%d" % d, 128, "float32") for d in range(1, 8)]):
     SCRATCH[_n] = ("sbuf", [128, _w], _t)
-for _h in "AB":
-    for _n, _w, _t in (("D1", 480, "bfloat16"), ("D2", 480, "bfloat16"), ("OF", 32, "uint16"), ("NX", 32, "float16"),
-                       ("TT", 32, "float32"), ("XT", 32, "float16"), ("WT", 32, "float32"), ("ZZ", 64, "float32")):
-        SCRATCH[_n + _h] = ("sbuf", [128, _w], _t)
-PSUM = ["PF", "PR", "PSA", "PSB", "EXA", "EXB", "ACA", "ACB"]
+for _b in range(3):
+    for _n, _w, _t in (("D1_", 320, "bfloat16"), ("D2_", 320, "bfloat16"), ("OF", 32, "uint16"), ("NX", 32, "float16"),
+                       ("TT", 24, "float32"), ("XT", 32, "float16"), ("WT", 32, "float32")):
+        SCRATCH["%s%d" % (_n, _b)] = ("sbuf", [128, _w], _t)
+PSUM = ["PF", "PR", "PS0", "PS1", "PS2", "EX", "AC"]
 for _n in PSUM:
     SCRATCH[_n] = ("psum", [128, 512], "float32")
 
@@ -124,7 +124,7 @@ def rank_program(g, core, T, topo):
     dma("S", "dN0", T.N0[:], T.nodes[:, 0:8], [], ["N0"])
     fill("Pi", T.Pi[:], 0)
     op("G", g.iota, [], ["IK"], T.IK[:], [[1, 1]], 0, 1)
-    op("G", g.iota, [], ["IR"], T.IR[:], [[1, 128]], 0, 0)
+    op("G", g.iota, [], ["IRf"], T.IRf[:], [[1, 128]], 0, 0, allow_small_or_imprecise_dtypes=True)
     for i in range(6):
         dma("S" if i < 3 else "A", "dP", T.Pi[i::16, :], T.pts[i % 3::3, :], [], ["Pi"], add=True)
     dma("S", "dSW", T.SKi[:], T.nodes[6::16, :], [], ["SKi"])
@@ -146,22 +146,21 @@ def rank_program(g, core, T, topo):
     dma("G", "dT1", T.TW[:, 1024:2048], T.nodes[:, 1024:2048], [], ["TWb"])
     op("G", g.iota, [], ["CJ"], T.CJ[:], [[0, 8], [-128, 2], [0, 8]], 255, -1, allow_small_or_imprecise_dtypes=True)
 
-    vc(["IK"], ["KF"], T.KF[:], T.IK[:])
     ts(["IK"], ["AI"], T.AI[:], T.IK[:], 15, None, ALU.bitwise_and)
-    vc(["IR"], ["IRf"], T.IRf[:], T.IR[:])
+    vc(["IK"], ["KF"], T.KF[:], T.IK[:])
+    ts(["IK"], ["HI16"], T.HI16[:], T.IK[:], 4, None, ALU.logical_shift_right)
     vc(["AI"], ["AF"], T.AF[:], T.AI[:])
     ts(["IK"], ["UI"], T.UI[:], T.IK[:], 5, None, ALU.logical_shift_right)
-    ts(["IK"], ["VI"], T.VI[:], T.IK[:], 1, 3, ALU.logical_shift_right, ALU.bitwise_and)
-    ts(["IK"], ["BI"], T.BI[:], T.IK[:], 24, None, ALU.bitwise_and)
-    ts(["IK"], ["GI"], T.GI[:], T.IK[:], 1, None, ALU.bitwise_and)
-    ts(["IK"], ["HI16"], T.HI16[:], T.IK[:], 4, None, ALU.logical_shift_right)
+    vc(["HI16"], ["P16"], T.P16[:], T.HI16[:])
     ts(["AF"], ["R1"], T.R1[:], T.AF[:], 2.5, None, ALU.is_gt)
     ts(["AF"], ["R2"], T.R2[:], T.AF[:], 5.5, -2.0, ALU.is_lt, ALU.mult)
-    ts(["AF"], ["VM"], T.VM[:], T.AF[:], 5.5, None, ALU.is_lt)
-    vc(["HI16"], ["P16"], T.P16[:], T.HI16[:])
-    tt(["R1", "R2"], ["R3"], T.R3[:], T.R1[:], T.R2[:], ALU.mult)
     ts(["IRf", "P16"], ["G8"], T.G8[:], T.IRf[:, 0:8], T.P16[:, 0:1], None, ALU.is_equal)
+    ts(["AF"], ["VM"], T.VM[:], T.AF[:], 5.5, None, ALU.is_lt)
+    tt(["R1", "R2"], ["R3"], T.R3[:], T.R1[:], T.R2[:], ALU.mult)
+    ts(["IK"], ["VI"], T.VI[:], T.IK[:], 1, 3, ALU.logical_shift_right, ALU.bitwise_and)
+    ts(["IK"], ["BI"], T.BI[:], T.IK[:], 24, None, ALU.bitwise_and)
     ts(["R3"], ["SG"], T.SG[:], T.R3[:], 1.0, None, ALU.add)
+    ts(["IK"], ["GI"], T.GI[:], T.IK[:], 1, None, ALU.bitwise_and)
     ts(["G8", "VM"], ["CM"], T.CM[:], T.G8[:], T.VM[:, 0:1], None, ALU.mult)
     ts(["Pi", "SG"], ["PL0"], T.PL[:, 0:256], T.Pi[:], T.SG[:, 0:1], None, ALU.mult)
     fill("AXm", T.AX[:, 0:M], 65536.0)
@@ -169,48 +168,48 @@ def rank_program(g, core, T, topo):
     fill("TWs", T.TW[:, M:MW], 4194304.0)
     vc(["SKi"], ["SKh"], T.SKh[:], T.SKi[:])
     ts(["Wi"], ["Wb"], T.Wb[:], T.Wi[:], 65536.0, None, ALU.add)
-    tt(["SKi", "SKh"], ["SKl"], T.SKl[:], T.SKi[:], T.SKh[:], ALU.subtract)
+    ts(["UI"], ["U2"], T.U2[:], T.UI[:], 2.0, None, ALU.mult)
     vc(["Wb"], ["Wh"], T.Wh[:], T.Wb[:])
+    tt(["SKi", "SKh"], ["SKl"], T.SKl[:], T.SKi[:], T.SKh[:], ALU.subtract)
     tt(["Wb", "Wh"], ["Wl"], T.Wl[:], T.Wb[:], T.Wh[:], ALU.subtract)
     wr["AX"] = []
     for i, n in enumerate(("SKh", "SKl", "Wh", "Wl")):
         dma("S", "dAX", T.AX[i::16, 0:M], T[n][:], [n, "AXm"], ["AX"], add=True)
     wr["AX"] = wr["AX"] + wr["AXm"] + wr["AXs"]
-    ts(["UI"], ["U2"], T.U2[:], T.UI[:], 2.0, None, ALU.mult)
     ts(["VI"], ["V32"], T.V32[:], T.VI[:], 32.0, None, ALU.mult)
     ts(["GI"], ["PEN0"], T.PEN0[:], T.GI[:], 1000.0, None, ALU.mult)
-    ts(["GI"], ["PEN1"], T.PEN1[:], T.GI[:], -1000.0, 1000.0, ALU.mult, ALU.add)
     tt(["U2", "V32"], ["UV"], T.UV[:], T.U2[:], T.V32[:], ALU.add)
+    ts(["GI"], ["PEN1"], T.PEN1[:], T.GI[:], -1000.0, 1000.0, ALU.mult, ALU.add)
     tt(["UV", "BI"], ["BASE"], T.BASE[:], T.UV[:], T.BI[:], ALU.add)
+    ts(["IRf", "KF"], ["TRI"], T.TRI[:], T.IRf[:], T.KF[:, 0:1], None, ALU.is_gt)
     tt(["BASE", "PEN0"], ["TG0"], T.TG0[:], T.BASE[:], T.PEN0[:], ALU.add)
     tt(["BASE", "PEN1"], ["TG1"], T.TG1[:], T.BASE[:], T.PEN1[:], ALU.add)
+    fill("ONE", T.ONE[:], 1.0)
     for x in (0, 1):
         for y in (0, 1):
             n = "L%d%d" % (x, y)
             ts(["IRf", "TG%d" % x], [n], T[n][:], T.IRf[:], float(-y), T["TG%d" % x][:, 0:1], ALU.add, ALU.is_equal)
-    ts(["IRf", "KF"], ["TRI"], T.TRI[:], T.IRf[:], T.KF[:, 0:1], None, ALU.is_gt)
-    fill("ONE", T.ONE[:], 1.0)
     fill("C1", T.C1[:], 0.0)
     fill("C2", T.C2[:], 0.0)
-    ts(["AF"], ["V4"], T.V4[:], T.AF[:], 4.0, None, ALU.is_equal)
-    ts(["AF"], ["V1"], T.V1[:], T.AF[:], 1.5, None, ALU.is_lt)
     ts(["AF"], ["W1"], T.W1[:], T.AF[:], 1.5, None, ALU.is_gt)
     ts(["AF"], ["W2"], T.W2[:], T.AF[:], 3.5, None, ALU.is_lt)
+    ts(["AF"], ["V4"], T.V4[:], T.AF[:], 4.0, None, ALU.is_equal)
+    ts(["AF"], ["V1"], T.V1[:], T.AF[:], 1.5, None, ALU.is_lt)
     tt(["W1", "W2"], ["W3"], T.W3[:], T.W1[:], T.W2[:], ALU.mult)
     await_("V", wr["C1"] + wr["C2"])
     for (n, q, col, f) in (("C1", 0, "VM", 4096.0), ("C1", 1, "VM", -2048.0), ("C1", 3, "VM", -2048.0),
                            ("C2", 0, "V4", 2.0 ** -16), ("C2", 1, "W3", 2.0 ** -6), ("C2", 2, "V1", 1.0),
                            ("C2", 3, "V4", 2.0 ** -6)):
         ts(["G8", col], [n], T[n][:, q::4], T.G8[:], T[col][:, 0:1], f, ALU.mult, ALU.mult)
-    for h in "AB":
-        fill("PS" + h, T["PS" + h][:, 0:128], 0.0)
-        fill("OF" + h, T["OF" + h][:], 1)
-        ts(["IRf"], ["NX" + h], T["NX" + h][:], T.IRf[:, 0:32], 0.0, 1.0, ALU.mult, ALU.add)
+    fill("F0z", T.F0[:, 0:1152], 0.0)
+    for b in "012":
+        fill("PS" + b, T["PS" + b][:, 0:96], 0.0)
+        fill("OF" + b, T["OF" + b][:], 1)
+        ts(["IRf"], ["NX" + b], T["NX" + b][:], T.IRf[:, 0:32], 0.0, 1.0, ALU.mult, ALU.add)
     ts(["IRf", "KF"], ["IDf"], T.IDf[:], T.IRf[:], T.KF[:, 0:1], None, ALU.is_equal)
     ts(["IRf", "KF"], ["IDh"], T.IDh[:], T.IRf[:], T.KF[:, 0:1], None, ALU.is_equal)
-    for b in range(4):
-        ts(["IRf"], ["HIT"], T.HIT[:, b * 128:b * 128 + 128], T.IRf[:], 0.0, None, ALU.mult)
-        ts(["IRf"], ["LOT"], T.LOT[:, b * 128:b * 128 + 128], T.IRf[:], 0.0, None, ALU.mult)
+    vc(["F0z"], ["HIT"], T.HIT[:], T.F0[:, 0:1152])
+    vc(["F0z"], ["LOT"], T.LOT[:], T.F0[:, 0:1152])
     act(["TWa", "SG"], ["TWa"], T.TW[:, 0:1024], T.TW[:, 0:1024], COPY, scale=T.SG[:, 0:1])
     act(["TWb", "SG"], ["TWb"], T.TW[:, 1024:M], T.TW[:, 1024:M], COPY, scale=T.SG[:, 0:1])
     TW = ["TWa", "TWb", "TWs"]
@@ -229,20 +228,20 @@ def rank_program(g, core, T, topo):
     for d in range(8):
         mm(["HB", "ONE"], ["PR"], T.PR[:, d * 16 + 8:d * 16 + 16], T.ONE[:], T.HB[:, d * 16:d * 16 + 8], False, d == 7)
 
-    def exchange(x, out, blocks):
+    def exchange(x, blocks):
         for b in range(blocks):
             for g0 in (0, 1):
                 for p4 in (0, 1):
                     n = "L%d%d" % (g0, p4)
-                    mm([x, n], [out], T[out][:, b * 32 + g0 * 16:b * 32 + g0 * 16 + 16], T[n][:],
+                    mm([x, n], ["EX"], T.EX[:, b * 32 + g0 * 16:b * 32 + g0 * 16 + 16], T[n][:],
                        T[x][:, b * 32 + p4 * 16:b * 32 + p4 * 16 + 16], p4 == 0, p4 == 1)
 
     tt(["PR", "MS"], ["SC"], T.SC[:], T.PR[:, 0:128], T.MS[:], ALU.add)
     op("V", v.transpose, ["SC"], ["SX"], T.SX[:], T.SC[:])
-    exchange("SX", "EXA", 4)
+    exchange("SX", 4)
     for d in range(8):
         fill("RZ%d" % d, T["RW%d" % d][:, (256 if d == 0 else 96):(288 if d == 0 else 128)], 0.0)
-    op("V", v.transpose, ["EXA"], ["ST"], T.ST[:], T.EXA[:, 0:128])
+    op("V", v.transpose, ["EX"], ["ST"], T.ST[:], T.EX[:, 0:128])
     vc(["ST"], ["SO"], T.SO[:], T.ST[:])
     for d in range(1, 8):
         vc(["PL0", "SO"], ["CP%d" % d], T.CP[:, (d - 1) * 256:d * 256].indirect(T.SO[:, d * 16:d * 16 + 16]), T.PL[:, 0:256])
@@ -253,103 +252,89 @@ def rank_program(g, core, T, topo):
         if d == 1:
             ts(["AX", "IRf"], ["AX0"], T.AX0[:], T.IRf[:], 0.0, T.AX[:, 0:1], ALU.mult, ALU.add)
 
-    def blocks(h):
-        n = HALF[h][1]
-        return [(b, b * 128, min(n, b * 128 + 128)) for b in range((n + 127) // 128)]
+    def blocks(b):
+        n = BATCH[b][1]
+        return [(k, k * 128, min(n, k * 128 + 128)) for k in range(3)]
 
-    def part(h, k):
-        return (0, 256) if k == 0 else (256, HALF[h][1])
+    def part(b, k):
+        return (0, 256) if k == 0 else (256, BATCH[b][1])
 
-    def sources(h, k):
-        if h == "A":
-            return ["PL0"] if k == 0 else ["PL1", "PL2"]
-        return ["PL3", "PL4", "PL5"] if k == 0 else ["PL5", "PL6", "PL7"]
+    def sources(lo, hi):
+        return (["PL0"] if lo < 256 else []) + ["PL%d" % d for d in range(1, 8) if lo < 256 + 96 * d and hi > 160 + 96 * d]
 
-    def visit_v(h, k, t):
-        lo, hi = part(h, k)
-        base = HALF[h][0]
-        out, pt = T["D1" + h][:, lo:hi], T.PL[:, base + lo:base + hi]
-        rs, ws = TW + sources(h, k), ["D1%s%d" % (h, k)]
+    def visit(b, k, t):
+        lo, hi = part(b, k)
+        base = BATCH[b][0]
+        offs = T["OF%d" % b][:, lo // 16:hi // 16]
+        out, pt = T["D1_%d" % b][:, lo:hi], T.PL[:, base + lo:base + hi]
+        rs, ws = TW + sources(base + lo, base + hi), ["D1_%d%d" % (b, k)]
         if t == 1:
             ts(rs, ws, out, pt, T.TW[:, 1:2], None, ALU.is_lt)
         else:
-            tt(rs + ["OF" + h], ws, out, T.TW[:].indirect(T["OF" + h][:, lo // 16:hi // 16]), pt, ALU.is_gt)
-
-    def visit_a(h, k):
-        lo, hi = part(h, k)
-        act(["AX", "OF" + h], ["D2%s%d" % (h, k)], T["D2" + h][:, lo:hi],
-            T.AX[:].indirect(T["OF" + h][:, lo // 16:hi // 16]), COPY)
-
-    def sums(h, k):
-        lo, hi = part(h, k)
-        for (b, x, y) in blocks(h):
+            tt(rs + ["OF%d" % b], ws, out, T.TW[:].indirect(offs), pt, ALU.is_gt)
+        act(["AX", "OF%d" % b], ["D2_%d%d" % (b, k)], T["D2_%d" % b][:, lo:hi], T.AX[:].indirect(offs), COPY)
+        for (j, x, y) in blocks(b):
             if lo <= x < hi:
-                out = T["PS" + h][0:y - x, b * 32:b * 32 + 32]
-                mm(["D2%s%d" % (h, k), "C2"], ["PS" + h], out, T["D2" + h][:, x:y], T.C2[:], True, False)
-                mm(["D1%s%d" % (h, k), "C1"], ["PS" + h], out, T["D1" + h][:, x:y], T.C1[:], False, True)
+                out = T["PS%d" % b][0:y - x, j * 32:j * 32 + 32]
+                mm(["D2_%d%d" % (b, k), "C2"], ["PS%d" % b], out, T["D2_%d" % b][:, x:y], T.C2[:], True, False)
+                mm(["D1_%d%d" % (b, k), "C1"], ["PS%d" % b], out, T["D1_%d" % b][:, x:y], T.C1[:], False, True)
 
-    def next_1(h):
-        ps = T["PS" + h]
-        tt(["PS" + h, "NX" + h], ["TT" + h], T["TT" + h][:], ps[:, 0:128:4], T["NX" + h][:], ALU.add)
-        tt(["PS" + h, "TT" + h], ["NX" + h], T["NX" + h][:], ps[:, 2:128:4], T["TT" + h][:], ALU.min)
-        op("V", v.transpose, ["NX" + h], ["XT" + h], T["XT" + h][:], T["NX" + h][:])
+    def weigh(b):
+        act(["PS%d" % b], ["ZZ%d" % b], T.ZZ[:, b * 48:b * 48 + 48], T["PS%d" % b][:, 1:96:2], RELU)
 
-    def next_2(h):
-        op("V", v.transpose, ["EX" + h], ["WT" + h], T["WT" + h][:], T["EX" + h][:, 0:32])
-        vc(["WT" + h], ["OF" + h], T["OF" + h][:], T["WT" + h][:])
+    def add_up(t):
+        mm(["ZZ0", "ZZ1", "ZZ2", "IDf"], ["AC"], T.AC[:, 0:144], T.IDf[:], T.ZZ[:], t == 0, t == STEPS)
 
-    def weigh(h):
-        act(["PS" + h], ["ZZ" + h], T["ZZ" + h][:], T["PS" + h][:, 1:128:2], RELU)
+    for b in range(3):
+        for (j, x, y) in blocks(b):
+            mm(["AX0", "C2"], ["PS%d" % b], T["PS%d" % b][0:y - x, j * 32:j * 32 + 32], T.AX0[:, 0:y - x], T.C2[:], True, True)
+        weigh(b)
+    add_up(0)
+    for s in range(3 * STEPS):
+        t, b = s // 3 + 1, s % 3
+        t1, b1 = (s - 1) // 3 + 1, (s - 1) % 3
+        t2, b2 = (s - 2) // 3 + 1, (s - 2) % 3
+        go1, go2 = s >= 1 and t1 < STEPS, s >= 2 and t2 < STEPS
+        visit(b, 0, t)
+        visit(b, 1, t)
+        ps, nx, tmp, xt = "PS%d" % b1, "NX%d" % b1, "TT%d" % b1, "XT%d" % b1
+        if go1:
+            tt([ps, nx], [tmp], T[tmp][:], T[ps][:, 0:96:4], T[nx][:, 0:24], ALU.add)
+        if go2:
+            op("V", v.transpose, ["EX"], ["WT%d" % b2], T["WT%d" % b2][:], T.EX[:, 0:32])
+        if go1:
+            tt([ps, tmp], [nx], T[nx][:, 0:24], T[ps][:, 2:96:4], T[tmp][:], ALU.min)
+        if go2:
+            vc(["WT%d" % b2], ["OF%d" % b2], T["OF%d" % b2][:], T["WT%d" % b2][:])
+        if go1:
+            op("V", v.transpose, [nx], [xt], T[xt][:], T[nx][:])
+            exchange(xt, 1)
+        if s >= 1:
+            weigh(b1)
+        if b1 == 2 and s >= 1:
+            add_up(t1)
+    weigh(2)
+    add_up(STEPS)
 
-    def add_up(h, t):
-        mm(["ZZ" + h, "IDf"], ["AC" + h], T["AC" + h][:, 0:64], T.IDf[:], T["ZZ" + h][:], t == 0, t == STEPS)
-
-    for h in "AB":
-        for (b, x, y) in blocks(h):
-            mm(["AX0", "C2"], ["PS" + h], T["PS" + h][0:y - x, b * 32:b * 32 + 32], T.AX0[:, 0:y - x], T.C2[:], True, True)
-        weigh(h)
-        add_up(h, 0)
-    for s in range(2 * STEPS):
-        t = s // 2 + 1
-        h, o = ("A", "B") if s % 2 == 0 else ("B", "A")
-        to = t if h == "B" else t - 1
-        visit_v(h, 0, t)
-        visit_a(h, 0)
-        if to >= 1:
-            if to < STEPS:
-                next_1(o)
-            weigh(o)
-        sums(h, 0)
-        if 1 <= to < STEPS:
-            exchange("XT" + o, "EX" + o, 1)
-        visit_v(h, 1, t)
-        visit_a(h, 1)
-        sums(h, 1)
-        if to >= 1:
-            if to < STEPS:
-                next_2(o)
-            add_up(o, to)
-    weigh("B")
-
-    def finish(h, tp):
-        ac = T["AC" + h]
-        vc(["AC" + h], ["SM"], T.SM[:], ac[:, 1:64:2])
-        tt(["AC" + h, "SM"], ["SS"], T.SS[:], ac[:, 0:64:2], T.SM[:], ALU.subtract)
-        vc(["SS"], ["HIT"], T.HIT[:, 0:512:16], T.SS[:])
-        tt(["SS", "HIT"], ["LOT"], T.LOT[:, 0:512:16], T.SS[:], T.HIT[:, 0:512:16], ALU.subtract)
-        for (b, x, y) in blocks(h):
-            mm(["HIT", "IDh"], [tp], T[tp][:, x:y], T.HIT[:, b * 128:b * 128 + 128], T.IDh[:, 0:y - x], True, False)
-            mm(["LOT", "IDh"], [tp], T[tp][:, x:y], T.LOT[:, b * 128:b * 128 + 128], T.IDh[:, 0:y - x], False, True)
-
-    finish("A", "PF")
-    act(["PF"], ["SA"], T.SA[:], T.PF[:, 256:448], COPY, scale=64.0)
-    act(["PF"], ["RV0"], T.RW0[:, 0:256], T.PF[:, 0:256], COPY, scale=64.0)
-    add_up("B", STEPS)
-    finish("B", "EXB")
-    act(["EXB"], ["SB"], T.SB[:], T.EXB[:, 0:480], COPY, scale=64.0)
+    vc(["AC"], ["SM"], T.SM[:], T.AC[:, 1:144:2])
+    tt(["AC", "SM"], ["SS"], T.SS[:], T.AC[:, 0:144:2], T.SM[:], ALU.subtract)
+    vc(["SS"], ["HIT"], T.HIT[:, 0:1152:16], T.SS[:])
+    tt(["SS", "HIT"], ["LOT"], T.LOT[:, 0:1152:16], T.SS[:], T.HIT[:, 0:1152:16], ALU.subtract)
+    for b in range(3):
+        ps = "PS%d" % b
+        for (j, x, y) in blocks(b):
+            c = (b * 3 + j) * 128
+            mm(["HIT", "IDh"], [ps], T[ps][:, x:y], T.HIT[:, c:c + 128], T.IDh[:, 0:y - x], True, False)
+            mm(["LOT", "IDh"], [ps], T[ps][:, x:y], T.LOT[:, c:c + 128], T.IDh[:, 0:y - x], False, True)
+        if b == 0:
+            act([ps], ["SA0"], T.SA[:, 0:64], T[ps][:, 256:320], COPY, scale=64.0)
+            act([ps], ["RV0"], T.RW0[:, 0:256], T[ps][:, 0:256], COPY, scale=64.0)
+        else:
+            lo, n = BATCH[b][0] - 256, BATCH[b][1]
+            act([ps], ["SA%d" % b], T.SA[:, lo:lo + n], T[ps][:, 0:n], COPY, scale=64.0)
     for d in range(1, 8):
-        src = T.SA[:, 96 * (d - 1):96 * d] if d < 3 else T.SB[:, 96 * (d - 3):96 * (d - 2)]
-        remote(T["RW%d" % d][:, 0:96], src, cores[(rank - d) % N], "rt%d" % d, ["SA" if d < 3 else "SB"])
+        tags = ["SA0", "SA1"] if d == 1 else ["SA1"] if d < 5 else ["SA2"]
+        remote(T["RW%d" % d][:, 0:96], T.SA[:, 96 * (d - 1):96 * d], cores[(rank - d) % N], "rt%d" % d, tags)
         total["rt%d" % d] = len(topo.engines(cores[(rank + d) % N], core))
         note((None, "rt%d" % d, total["rt%d" % d]), [], ["RV%d" % d])
     ts(["PR"], ["Q1"], T.Q1[:], T.PR[:, 0:128], -96.0, None, ALU.add)
@@ -357,14 +342,22 @@ def rank_program(g, core, T, topo):
     tt(["Q1", "HB"], ["GQ"], T.GQ[:, 16:128], T.Q1[:, 16:128], T.HB[:, 16:128], ALU.mult)
     op("V", v.tensor_tensor, ["JT", "HB"], ["GQ"], T.GQ[:, 0:16], T.JT[:], T.HB[:, 0:16], ALU.mult, add=True)
     op("V", v.transpose, ["GQ"], ["GX"], T.GX[:], T.GQ[:])
-    exchange("GX", "EXA", 4)
-    op("V", v.transpose, ["EXA"], ["GT"], T.GT[:], T.EXA[:, 0:128])
+    exchange("GX", 4)
+    op("V", v.transpose, ["EX"], ["GT"], T.GT[:], T.EX[:, 0:128])
     ts(["GT"], ["GO0"], T.GO[:, 0:16], T.GT[:, 0:16], 256.0, None, ALU.add)
     ts(["GT"], ["GO1"], T.GO[:, 16:128], T.GT[:, 16:128], 96.0, None, ALU.add)
-    vc(["RV0", "RZ0", "GO0"], ["Y0"], T.Y0[:], T.RW0[:].indirect(T.GO[:, 0:16]))
-    for d in range(1, 8):
-        x, y = ("Y0", "Y1") if d % 2 else ("Y1", "Y0")
-        tt([x, "RV%d" % d, "RZ%d" % d, "GO1"], [y], T[y][:], T["RW%d" % d][:].indirect(T.GO[:, d * 16:d * 16 + 16]), T[x][:], ALU.add)
+
+    def sums_of(d):
+        return T["RW%d" % d][:].indirect(T.GO[:, d * 16:d * 16 + 16]), ["RV%d" % d, "RZ%d" % d, "GO%d" % min(d, 1)]
+
+    for d in range(3):
+        win, rs = sums_of(d)
+        act(rs, ["A%d" % d], T["A%d" % d][:], win, COPY)
+    for d, x, y in ((3, "A0", "Y0"), (4, "A1", "Y1"), (5, "A2", "Y2"), (6, "Y0", "A0"), (7, "Y1", "A1")):
+        win, rs = sums_of(d)
+        tt(rs + [x], [y], T[y][:], win, T[x][:], ALU.add)
+    tt(["A0", "Y2"], ["Y0"], T.Y0[:], T.A0[:], T.Y2[:], ALU.add)
+    tt(["Y0", "A1"], ["Y1"], T.Y1[:], T.Y0[:], T.A1[:], ALU.add)
     dma("S", "dY", T.y[:, :], T.Y1[0::16, :], ["Y1"], ["y"])
     for sem in sorted(total):
         if max([seen.get((q, sem), 0) for q in queue]) < total[sem]:

@@ -18,12 +18,12 @@ for _n, _w, _t in (
         + [(n, 128, "float32") for n in "CJ IRf IDf Wb MS ST Q1 GT".split()]
         + [(n, 128, "bfloat16") for n in "TRI ONE AX0 SKh SKl Wh Wl HB NB".split()]
         + [(n, 128, "float16") for n in "IDh L00 L01 L10 L11 SC SX GQ GX".split()]
-        + [(n, 256, "float32") for n in "A0 A1 A2 Y0 Y1 Y2".split()]
+        + [(n, 256, "float32") for n in "A0 A1 A2 Y0 Y1 Y2 Y3".split()]
         + [("SO", 128, "uint16"), ("GO", 128, "uint16"), ("G8", 8, "float32"), ("CM", 8, "bfloat16"),
            ("C1", 32, "bfloat16"), ("C2", 32, "bfloat16"), ("JT", 16, "float32"), ("N0", 8, "int32"),
            ("BXi", 8, "int32"), ("BX", 8, "float32"), ("Pi", 256, "int32"), ("PL", 928, "float32"),
            ("TW", MW, "float32"), ("AX", MW, "bfloat16"), ("F0", 2048, "bfloat16"), ("CP", 7 * 256, "float32"),
-           ("HIT", 1152, "float16"), ("LOT", 1152, "float16"), ("SM", 72, "float32"), ("SS", 72, "float32"),
+           ("HIT", 1152, "float16"), ("LOT", 1152, "float16"), ("EE", 144, "float32"), ("SS", 72, "float32"),
            ("SA", 672, "float32"), ("ZZ", 144, "float32"), ("RW0", 288, "float32")]
         + [("RW%d" % d, 128, "float32") for d in range(1, 8)]):
     SCRATCH[_n] = ("sbuf", [128, _w], _t)
@@ -31,7 +31,7 @@ for _b in range(3):
     for _n, _w, _t in (("D1_", 320, "bfloat16"), ("D2_", 320, "bfloat16"), ("OF", 32, "uint16"), ("NX", 32, "float16"),
                        ("TT", 24, "float32"), ("XT", 32, "float16"), ("WT", 32, "float32")):
         SCRATCH["%s%d" % (_n, _b)] = ("sbuf", [128, _w], _t)
-PSUM = ["PF", "PR", "PS0", "PS1", "PS2", "EX", "AC"]
+PSUM = ["PF", "PR", "PQ", "PS0", "PS1", "PS2", "EX", "AC"]
 for _n in PSUM:
     SCRATCH[_n] = ("psum", [128, 512], "float32")
 
@@ -46,7 +46,7 @@ def rank_program(g, core, T, topo):
         return
     cores = T.cores
     queue = {"V": g.vector, "A": g.scalar, "P": g.tensor, "G": g, "S": g.sync}
-    total = {}
+    total = {"ls": 0}
     seen = {}
     wr, rd = {}, {}
 
@@ -95,12 +95,6 @@ def rank_program(g, core, T, topo):
         queue[q].dma_start(out, in_).then_inc(T.sem[sem], 16)
         note((None, sem, total[sem]), reads, writes, add)
 
-    def remote(out_ap, in_ap, dst, rsem, reads):
-        deps("G", reads, [])
-        rid, pid, _ = topo.addr(dst)
-        total["ls"] = total.get("ls", 0) + len(topo.engines(core, dst))
-        g.remote_dma(out_ap, in_ap, T.sem[rsem], T.sem.ls, pid, rid, topo.mask(core, dst))
-
     v, a, p = g.vector, g.scalar, g.tensor
 
     def ts(reads, writes, out, in0, s1, s2, *ops):
@@ -111,6 +105,9 @@ def rank_program(g, core, T, topo):
 
     def vc(reads, writes, out, in_):
         op("V", v.tensor_copy, reads, writes, out, in_)
+
+    def turn(x, y, out, in_):
+        op("V", v.transpose, [x], [y], out, in_)
 
     def fill(tag, ap, c):
         op("V", v.memset, [], [tag], ap, c)
@@ -136,7 +133,7 @@ def rank_program(g, core, T, topo):
         rid, pid, _ = topo.addr(dcore)
         ids.append(DstId(rid=rid, pnc=pid))
     lanes = len(topo.engines(core, dsts[0]))
-    total["ls"] = lanes
+    total["ls"] += lanes
     g.remote_dma_fused([RemoteDMATransfer(
         dst_ids=ids, dma_engine_mask=topo.mask(core, dsts[0]), remote_sem=T.sem.box, srcs=[T.N0[:, 0:1]],
         dsts=[T.BXi[:, N - e:N - e + 1] for e in range(1, N)])], local_sem=T.sem.ls)
@@ -145,6 +142,7 @@ def rank_program(g, core, T, topo):
     dma("G", "dT0", T.TW[:, 0:1024], T.nodes[:, 0:1024], [], ["TWa"])
     dma("G", "dT1", T.TW[:, 1024:2048], T.nodes[:, 1024:2048], [], ["TWb"])
     op("G", g.iota, [], ["CJ"], T.CJ[:], [[0, 8], [-128, 2], [0, 8]], 255, -1, allow_small_or_imprecise_dtypes=True)
+    op("G", g.iota, [], ["AXm"], T.AX[:, 0:M], [[0, M]], 65536, 0, allow_small_or_imprecise_dtypes=True)
 
     ts(["IK"], ["AI"], T.AI[:], T.IK[:], 15, None, ALU.bitwise_and)
     vc(["IK"], ["KF"], T.KF[:], T.IK[:])
@@ -162,128 +160,172 @@ def rank_program(g, core, T, topo):
     ts(["R3"], ["SG"], T.SG[:], T.R3[:], 1.0, None, ALU.add)
     ts(["IK"], ["GI"], T.GI[:], T.IK[:], 1, None, ALU.bitwise_and)
     ts(["G8", "VM"], ["CM"], T.CM[:], T.G8[:], T.VM[:, 0:1], None, ALU.mult)
-    ts(["Pi", "SG"], ["PL0"], T.PL[:, 0:256], T.Pi[:], T.SG[:, 0:1], None, ALU.mult)
-    fill("AXm", T.AX[:, 0:M], 65536.0)
-    fill("AXs", T.AX[:, M:MW], 1024.0)
-    fill("TWs", T.TW[:, M:MW], 4194304.0)
-    vc(["SKi"], ["SKh"], T.SKh[:], T.SKi[:])
-    ts(["Wi"], ["Wb"], T.Wb[:], T.Wi[:], 65536.0, None, ALU.add)
     ts(["UI"], ["U2"], T.U2[:], T.UI[:], 2.0, None, ALU.mult)
-    vc(["Wb"], ["Wh"], T.Wh[:], T.Wb[:])
-    tt(["SKi", "SKh"], ["SKl"], T.SKl[:], T.SKi[:], T.SKh[:], ALU.subtract)
-    tt(["Wb", "Wh"], ["Wl"], T.Wl[:], T.Wb[:], T.Wh[:], ALU.subtract)
-    wr["AX"] = []
-    for i, n in enumerate(("SKh", "SKl", "Wh", "Wl")):
-        dma("S", "dAX", T.AX[i::16, 0:M], T[n][:], [n, "AXm"], ["AX"], add=True)
-    wr["AX"] = wr["AX"] + wr["AXm"] + wr["AXs"]
     ts(["VI"], ["V32"], T.V32[:], T.VI[:], 32.0, None, ALU.mult)
     ts(["GI"], ["PEN0"], T.PEN0[:], T.GI[:], 1000.0, None, ALU.mult)
-    tt(["U2", "V32"], ["UV"], T.UV[:], T.U2[:], T.V32[:], ALU.add)
     ts(["GI"], ["PEN1"], T.PEN1[:], T.GI[:], -1000.0, 1000.0, ALU.mult, ALU.add)
-    tt(["UV", "BI"], ["BASE"], T.BASE[:], T.UV[:], T.BI[:], ALU.add)
+    tt(["U2", "V32"], ["UV"], T.UV[:], T.U2[:], T.V32[:], ALU.add)
     ts(["IRf", "KF"], ["TRI"], T.TRI[:], T.IRf[:], T.KF[:, 0:1], None, ALU.is_gt)
+    tt(["UV", "BI"], ["BASE"], T.BASE[:], T.UV[:], T.BI[:], ALU.add)
+    fill("ONE", T.ONE[:], 1.0)
     tt(["BASE", "PEN0"], ["TG0"], T.TG0[:], T.BASE[:], T.PEN0[:], ALU.add)
     tt(["BASE", "PEN1"], ["TG1"], T.TG1[:], T.BASE[:], T.PEN1[:], ALU.add)
-    fill("ONE", T.ONE[:], 1.0)
+    ts(["Pi", "SG"], ["PL0"], T.PL[:, 0:256], T.Pi[:], T.SG[:, 0:1], None, ALU.mult)
     for x in (0, 1):
         for y in (0, 1):
             n = "L%d%d" % (x, y)
             ts(["IRf", "TG%d" % x], [n], T[n][:], T.IRf[:], float(-y), T["TG%d" % x][:, 0:1], ALU.add, ALU.is_equal)
+    vc(["SKi"], ["SKh"], T.SKh[:], T.SKi[:])
+    ts(["Wi"], ["Wb"], T.Wb[:], T.Wi[:], 65536.0, None, ALU.add)
     fill("C1", T.C1[:], 0.0)
+    vc(["Wb"], ["Wh"], T.Wh[:], T.Wb[:])
+    tt(["SKi", "SKh"], ["SKl"], T.SKl[:], T.SKi[:], T.SKh[:], ALU.subtract)
     fill("C2", T.C2[:], 0.0)
+    tt(["Wb", "Wh"], ["Wl"], T.Wl[:], T.Wb[:], T.Wh[:], ALU.subtract)
+    wr["AX"] = []
+    for i, n in enumerate(("SKh", "SKl", "Wh", "Wl")):
+        dma("S", "dAX", T.AX[i::16, 0:M], T[n][:], [n, "AXm"], ["AX"], add=True)
     ts(["AF"], ["W1"], T.W1[:], T.AF[:], 1.5, None, ALU.is_gt)
     ts(["AF"], ["W2"], T.W2[:], T.AF[:], 3.5, None, ALU.is_lt)
     ts(["AF"], ["V4"], T.V4[:], T.AF[:], 4.0, None, ALU.is_equal)
     ts(["AF"], ["V1"], T.V1[:], T.AF[:], 1.5, None, ALU.is_lt)
     tt(["W1", "W2"], ["W3"], T.W3[:], T.W1[:], T.W2[:], ALU.mult)
+    fill("AXs", T.AX[:, M:MW], 1024.0)
+    wr["AX"] = wr["AX"] + wr["AXm"] + wr["AXs"]
     await_("V", wr["C1"] + wr["C2"])
     for (n, q, col, f) in (("C1", 0, "VM", 4096.0), ("C1", 1, "VM", -2048.0), ("C1", 3, "VM", -2048.0),
                            ("C2", 0, "V4", 2.0 ** -16), ("C2", 1, "W3", 2.0 ** -6), ("C2", 2, "V1", 1.0),
                            ("C2", 3, "V4", 2.0 ** -6)):
         ts(["G8", col], [n], T[n][:, q::4], T.G8[:], T[col][:, 0:1], f, ALU.mult, ALU.mult)
-    fill("F0z", T.F0[:, 0:1152], 0.0)
-    for b in "012":
-        fill("PS" + b, T["PS" + b][:, 0:96], 0.0)
-        fill("OF" + b, T["OF" + b][:], 1)
-        ts(["IRf"], ["NX" + b], T["NX" + b][:], T.IRf[:, 0:32], 0.0, 1.0, ALU.mult, ALU.add)
-    ts(["IRf", "KF"], ["IDf"], T.IDf[:], T.IRf[:], T.KF[:, 0:1], None, ALU.is_equal)
-    ts(["IRf", "KF"], ["IDh"], T.IDh[:], T.IRf[:], T.KF[:, 0:1], None, ALU.is_equal)
-    vc(["F0z"], ["HIT"], T.HIT[:], T.F0[:, 0:1152])
-    vc(["F0z"], ["LOT"], T.LOT[:], T.F0[:, 0:1152])
+    fill("TWs", T.TW[:, M:MW], 4194304.0)
     act(["TWa", "SG"], ["TWa"], T.TW[:, 0:1024], T.TW[:, 0:1024], COPY, scale=T.SG[:, 0:1])
     act(["TWb", "SG"], ["TWb"], T.TW[:, 1024:M], T.TW[:, 1024:M], COPY, scale=T.SG[:, 0:1])
     TW = ["TWa", "TWb", "TWs"]
 
-    ts(["N0", "SG"], ["BX0"], T.BX[:, 0:1], T.N0[:, 0:1], T.SG[:, 0:1], None, ALU.mult)
-    ts(["BXi", "SG"], ["BX1"], T.BX[:, 1:8], T.BXi[:, 1:8], T.SG[:, 0:1], None, ALU.mult)
-    for d in list(range(1, 8)) + [0]:
+    COUNT, POS, EXCH = ["PF", "AC"], ["PR", "PQ"], ["EX", "PS0"]
+
+    def inside(d):
         ts(["PL0", "BX%d" % min(d, 1)], ["F0_%d" % d], T.F0[:, d * 256:d * 256 + 256], T.PL[:, 0:256], T.BX[:, d:d + 1], None, ALU.is_lt)
+        ps = COUNT[d // 4]
         for jb in (0, 1):
             c = d * 16 + jb * 8
-            mm(["F0_%d" % d, "CM"], ["PF"], T.PF[:, c:c + 8], T.F0[:, d * 256 + jb * 128:d * 256 + jb * 128 + 128], T.CM[:], True, True)
-    ts(["PF"], ["HB"], T.HB[:], T.PF[:, 0:128], 0.5, None, ALU.is_lt)
-    ts(["PF"], ["NB"], T.NB[:], T.PF[:, 0:128], 0.5, None, ALU.is_gt)
-    tt(["NB", "CJ"], ["MS"], T.MS[:], T.NB[:], T.CJ[:], ALU.mult)
-    mm(["HB", "TRI"], ["PR"], T.PR[:, 0:128], T.TRI[:], T.HB[:], True, False)
-    for d in range(8):
-        mm(["HB", "ONE"], ["PR"], T.PR[:, d * 16 + 8:d * 16 + 16], T.ONE[:], T.HB[:, d * 16:d * 16 + 8], False, d == 7)
+            mm(["F0_%d" % d, "CM"], [ps], T[ps][:, c % 64:c % 64 + 8],
+               T.F0[:, d * 256 + jb * 128:d * 256 + jb * 128 + 128], T.CM[:], True, True)
 
-    def exchange(x, blocks):
-        for b in range(blocks):
+    def cols(n, k):
+        return T[n][:, 64 * k:64 * k + 64]
+
+    def hits(k):
+        ts([COUNT[k]], ["HB%d" % k], cols("HB", k), T[COUNT[k]][:, 0:64], 0.5, None, ALU.is_lt)
+        ts([COUNT[k]], ["NB%d" % k], cols("NB", k), T[COUNT[k]][:, 0:64], 0.5, None, ALU.is_gt)
+        ps = POS[k]
+        mm(["HB%d" % k, "TRI"], [ps], T[ps][:, 0:64], T.TRI[:], cols("HB", k), True, False)
+        for d in range(4):
+            mm(["HB%d" % k, "ONE"], [ps], T[ps][:, d * 16 + 8:d * 16 + 16], T.ONE[:],
+               T.HB[:, k * 64 + d * 16:k * 64 + d * 16 + 8], False, d == 3)
+
+    def away(k):
+        tt(["NB%d" % k, "CJ"], ["MS%d" % k], cols("MS", k), cols("NB", k), cols("CJ", k), ALU.mult)
+
+    def place(k):
+        tt([POS[k], "MS%d" % k], ["SC%d" % k], cols("SC", k), T[POS[k]][:, 0:64], cols("MS", k), ALU.add)
+
+    def exchange(x, ps, c, n):
+        tag, buf = x
+        for b in range(n):
             for g0 in (0, 1):
                 for p4 in (0, 1):
-                    n = "L%d%d" % (g0, p4)
-                    mm([x, n], ["EX"], T.EX[:, b * 32 + g0 * 16:b * 32 + g0 * 16 + 16], T[n][:],
-                       T[x][:, b * 32 + p4 * 16:b * 32 + p4 * 16 + 16], p4 == 0, p4 == 1)
+                    m = "L%d%d" % (g0, p4)
+                    mm([tag, m], [ps], T[ps][:, b * 32 + g0 * 16:b * 32 + g0 * 16 + 16], T[m][:],
+                       T[buf][:, c + b * 32 + p4 * 16:c + b * 32 + p4 * 16 + 16], p4 == 0, p4 == 1)
 
-    tt(["PR", "MS"], ["SC"], T.SC[:], T.PR[:, 0:128], T.MS[:], ALU.add)
-    op("V", v.transpose, ["SC"], ["SX"], T.SX[:], T.SC[:])
-    exchange("SX", 4)
-    for d in range(8):
-        fill("RZ%d" % d, T["RW%d" % d][:, (256 if d == 0 else 96):(288 if d == 0 else 128)], 0.0)
-    op("V", v.transpose, ["EX"], ["ST"], T.ST[:], T.EX[:, 0:128])
-    vc(["ST"], ["SO"], T.SO[:], T.ST[:])
-    for d in range(1, 8):
-        vc(["PL0", "SO"], ["CP%d" % d], T.CP[:, (d - 1) * 256:d * 256].indirect(T.SO[:, d * 16:d * 16 + 16]), T.PL[:, 0:256])
-        remote(T.PL[:, 256 + 96 * (d - 1):256 + 96 * d], T.CP[:, (d - 1) * 256:(d - 1) * 256 + 96],
-               cores[(rank + d) % N], "pt%d" % d, ["CP%d" % d] + ["RZ%d" % k for k in range(8)])
+    def swap(k):
+        turn("SC%d" % k, "SX%d" % k, cols("SX", k), cols("SC", k))
+        exchange(("SX%d" % k, "SX"), EXCH[k], 64 * k, 2)
+
+    def back(k):
+        turn(EXCH[k], "ST%d" % k, cols("ST", k), T[EXCH[k]][:, 0:64])
+
+    def list_(k):
+        vc(["ST%d" % k], ["SO%d" % k], cols("SO", k), cols("ST", k))
+
+    def scatter(d):
+        vc(["PL0", "SO%d" % (d // 4)], ["CP%d" % d], T.CP[:, (d - 1) * 256:d * 256].indirect(T.SO[:, d * 16:d * 16 + 16]), T.PL[:, 0:256])
+        deps("G", ["CP%d" % d] + ["RZ%d" % k for k in range(8)], [])
+        dst = cores[(rank + d) % N]
+        rid, pid, _ = topo.addr(dst)
+        total["ls"] += len(topo.engines(core, dst))
+        g.remote_dma(T.PL[:, 256 + 96 * (d - 1):256 + 96 * d], T.CP[:, (d - 1) * 256:(d - 1) * 256 + 96],
+                     T.sem["pt%d" % d], T.sem.ls, pid, rid, topo.mask(core, dst))
         total["pt%d" % d] = len(topo.engines(cores[(rank - d) % N], core))
         note((None, "pt%d" % d, total["pt%d" % d]), [], ["PL%d" % d])
-        if d == 1:
+
+    def zero_slot(d):
+        fill("RZ%d" % d, T["RW%d" % d][:, (256 if d == 0 else 96):(288 if d == 0 else 128)], 0.0)
+
+    ts(["N0", "SG"], ["BX0"], T.BX[:, 0:1], T.N0[:, 0:1], T.SG[:, 0:1], None, ALU.mult)
+    ts(["BXi", "SG"], ["BX1"], T.BX[:, 1:8], T.BXi[:, 1:8], T.SG[:, 0:1], None, ALU.mult)
+    for d in (1, 2, 3, 0, 4):
+        inside(d)
+    hits(0)
+    inside(5)
+    away(0)
+    inside(6)
+    place(0)
+    inside(7)
+    swap(0)
+    hits(1)
+    away(1)
+    for d in range(8):
+        zero_slot(d)
+    back(0)
+    place(1)
+    list_(0)
+    fill("PS1", T.PS1[:, 0:96], 0.0)
+    swap(1)
+    scatter(1)
+    back(1)
+    scatter(2)
+    list_(1)
+    scatter(3)
+    for d in range(4, 8):
+        scatter(d)
+        if d == 4:
             ts(["AX", "IRf"], ["AX0"], T.AX0[:], T.IRf[:], 0.0, T.AX[:, 0:1], ALU.mult, ALU.add)
+            fill("PS0", T.PS0[:, 0:96], 0.0)
+            fill("PS2", T.PS2[:, 0:96], 0.0)
+            ts(["IRf", "KF"], ["IDf"], T.IDf[:], T.IRf[:], T.KF[:, 0:1], None, ALU.is_equal)
+            for b in "012":
+                fill("OF" + b, T["OF" + b][:], 1)
+                ts(["IRf"], ["NX" + b], T["NX" + b][:], T.IRf[:, 0:32], 0.0, 1.0, ALU.mult, ALU.add)
 
     def blocks(b):
         n = BATCH[b][1]
         return [(k, k * 128, min(n, k * 128 + 128)) for k in range(3)]
 
-    def part(b, k):
-        return (0, 256) if k == 0 else (256, BATCH[b][1])
-
     def sources(lo, hi):
         return (["PL0"] if lo < 256 else []) + ["PL%d" % d for d in range(1, 8) if lo < 256 + 96 * d and hi > 160 + 96 * d]
 
-    def visit(b, k, t):
-        lo, hi = part(b, k)
-        base = BATCH[b][0]
-        offs = T["OF%d" % b][:, lo // 16:hi // 16]
-        out, pt = T["D1_%d" % b][:, lo:hi], T.PL[:, base + lo:base + hi]
-        rs, ws = TW + sources(base + lo, base + hi), ["D1_%d%d" % (b, k)]
+    def visit(b, t):
+        lo, n = BATCH[b]
+        offs = T["OF%d" % b][:, 0:n // 16]
+        out, pt = T["D1_%d" % b][:, 0:n], T.PL[:, lo:lo + n]
+        rs, ws = TW + sources(lo, lo + n), ["D1_%d" % b]
         if t == 1:
             ts(rs, ws, out, pt, T.TW[:, 1:2], None, ALU.is_lt)
         else:
             tt(rs + ["OF%d" % b], ws, out, T.TW[:].indirect(offs), pt, ALU.is_gt)
-        act(["AX", "OF%d" % b], ["D2_%d%d" % (b, k)], T["D2_%d" % b][:, lo:hi], T.AX[:].indirect(offs), COPY)
+        act(["AX", "OF%d" % b], ["D2_%d" % b], T["D2_%d" % b][:, 0:n], T.AX[:].indirect(offs), COPY)
         for (j, x, y) in blocks(b):
-            if lo <= x < hi:
-                out = T["PS%d" % b][0:y - x, j * 32:j * 32 + 32]
-                mm(["D2_%d%d" % (b, k), "C2"], ["PS%d" % b], out, T["D2_%d" % b][:, x:y], T.C2[:], True, False)
-                mm(["D1_%d%d" % (b, k), "C1"], ["PS%d" % b], out, T["D1_%d" % b][:, x:y], T.C1[:], False, True)
+            out = T["PS%d" % b][0:y - x, j * 32:j * 32 + 32]
+            mm(["D2_%d" % b, "C2"], ["PS%d" % b], out, T["D2_%d" % b][:, x:y], T.C2[:], True, False)
+            mm(["D1_%d" % b, "C1"], ["PS%d" % b], out, T["D1_%d" % b][:, x:y], T.C1[:], False, True)
 
     def weigh(b):
         act(["PS%d" % b], ["ZZ%d" % b], T.ZZ[:, b * 48:b * 48 + 48], T["PS%d" % b][:, 1:96:2], RELU)
 
     def add_up(t):
-        mm(["ZZ0", "ZZ1", "ZZ2", "IDf"], ["AC"], T.AC[:, 0:144], T.IDf[:], T.ZZ[:], t == 0, t == STEPS)
+        mm(["ZZ0", "ZZ1", "ZZ2", "IDf"], ["AC"], T.AC[:, 0:144], T.IDf[:], T.ZZ[:], t == 0, t == STEPS - 1)
 
     for b in range(3):
         for (j, x, y) in blocks(b):
@@ -295,70 +337,114 @@ def rank_program(g, core, T, topo):
         t1, b1 = (s - 1) // 3 + 1, (s - 1) % 3
         t2, b2 = (s - 2) // 3 + 1, (s - 2) % 3
         go1, go2 = s >= 1 and t1 < STEPS, s >= 2 and t2 < STEPS
-        visit(b, 0, t)
-        visit(b, 1, t)
+        visit(b, t)
         ps, nx, tmp, xt = "PS%d" % b1, "NX%d" % b1, "TT%d" % b1, "XT%d" % b1
         if go1:
             tt([ps, nx], [tmp], T[tmp][:], T[ps][:, 0:96:4], T[nx][:, 0:24], ALU.add)
         if go2:
-            op("V", v.transpose, ["EX"], ["WT%d" % b2], T["WT%d" % b2][:], T.EX[:, 0:32])
+            turn("EX", "WT%d" % b2, T["WT%d" % b2][:], T.EX[:, 0:32])
         if go1:
             tt([ps, tmp], [nx], T[nx][:, 0:24], T[ps][:, 2:96:4], T[tmp][:], ALU.min)
         if go2:
             vc(["WT%d" % b2], ["OF%d" % b2], T["OF%d" % b2][:], T["WT%d" % b2][:])
         if go1:
-            op("V", v.transpose, [nx], [xt], T[xt][:], T[nx][:])
-            exchange(xt, 1)
+            turn(nx, xt, T[xt][:], T[nx][:])
+            exchange((xt, xt), "EX", 0, 1)
         if s >= 1:
             weigh(b1)
-        if b1 == 2 and s >= 1:
+        if b1 == 2 and s >= 1 and t1 < STEPS:
             add_up(t1)
+        if s == 0:
+            fill("F0z", T.F0[:, 0:1152], 0.0)
+            ts(["IRf", "KF"], ["IDh"], T.IDh[:], T.IRf[:], T.KF[:, 0:1], None, ALU.is_equal)
+        if s == 1:
+            vc(["F0z"], ["HITz"], T.HIT[:], T.F0[:, 0:1152])
+        if s == 2:
+            vc(["F0z"], ["LOTz"], T.LOT[:], T.F0[:, 0:1152])
     weigh(2)
-    add_up(STEPS)
 
-    vc(["AC"], ["SM"], T.SM[:], T.AC[:, 1:144:2])
-    tt(["AC", "SM"], ["SS"], T.SS[:], T.AC[:, 0:144:2], T.SM[:], ALU.subtract)
-    vc(["SS"], ["HIT"], T.HIT[:, 0:1152:16], T.SS[:])
-    tt(["SS", "HIT"], ["LOT"], T.LOT[:, 0:1152:16], T.SS[:], T.HIT[:, 0:1152:16], ALU.subtract)
-    for b in range(3):
+    def last_1(b):
+        x = slice(b * 48, b * 48 + 48)
+        tt(["AC", "ZZ%d" % b], ["EE%d" % b], T.EE[:, x], T.AC[:, x], T.ZZ[:, x], ALU.add)
+
+    def last_2(b):
+        tt(["EE%d" % b], ["SS%d" % b], T.SS[:, b * 24:b * 24 + 24], T.EE[:, b * 48:b * 48 + 48:2],
+           T.EE[:, b * 48 + 1:b * 48 + 48:2], ALU.subtract)
+
+    def last_3(b):
+        vc(["SS%d" % b, "HITz"], ["HIT%d" % b], T.HIT[:, b * 384:b * 384 + 384:16], T.SS[:, b * 24:b * 24 + 24])
+
+    def last_4(b):
+        tt(["SS%d" % b, "HIT%d" % b, "LOTz"], ["LOT%d" % b], T.LOT[:, b * 384:b * 384 + 384:16],
+           T.SS[:, b * 24:b * 24 + 24], T.HIT[:, b * 384:b * 384 + 384:16], ALU.subtract)
+
+    def rows(b):
         ps = "PS%d" % b
         for (j, x, y) in blocks(b):
             c = (b * 3 + j) * 128
-            mm(["HIT", "IDh"], [ps], T[ps][:, x:y], T.HIT[:, c:c + 128], T.IDh[:, 0:y - x], True, False)
-            mm(["LOT", "IDh"], [ps], T[ps][:, x:y], T.LOT[:, c:c + 128], T.IDh[:, 0:y - x], False, True)
+            mm(["HIT%d" % b, "IDh"], [ps], T[ps][:, x:y], T.HIT[:, c:c + 128], T.IDh[:, 0:y - x], True, False)
+            mm(["LOT%d" % b, "IDh"], [ps], T[ps][:, x:y], T.LOT[:, c:c + 128], T.IDh[:, 0:y - x], False, True)
         if b == 0:
             act([ps], ["SA0"], T.SA[:, 0:64], T[ps][:, 256:320], COPY, scale=64.0)
             act([ps], ["RV0"], T.RW0[:, 0:256], T[ps][:, 0:256], COPY, scale=64.0)
         else:
             lo, n = BATCH[b][0] - 256, BATCH[b][1]
             act([ps], ["SA%d" % b], T.SA[:, lo:lo + n], T[ps][:, 0:n], COPY, scale=64.0)
-    for d in range(1, 8):
-        tags = ["SA0", "SA1"] if d == 1 else ["SA1"] if d < 5 else ["SA2"]
-        remote(T["RW%d" % d][:, 0:96], T.SA[:, 96 * (d - 1):96 * d], cores[(rank - d) % N], "rt%d" % d, tags)
-        total["rt%d" % d] = len(topo.engines(cores[(rank + d) % N], core))
-        note((None, "rt%d" % d, total["rt%d" % d]), [], ["RV%d" % d])
-    ts(["PR"], ["Q1"], T.Q1[:], T.PR[:, 0:128], -96.0, None, ALU.add)
+
+    def send(ds, tags, cuts):
+        deps("G", tags, [])
+        trs = []
+        for i, d in enumerate(ds):
+            dst = cores[(rank - d) % N]
+            rid, pid, _ = topo.addr(dst)
+            es = topo.engines(core, dst)[cuts[i]:cuts[i + 1]]
+            trs.append(RemoteDMATransfer(
+                dst_ids=[DstId(rid=rid, pnc=pid)], dma_engine_mask=sum(1 << e for e in es), remote_sem=T.sem["rt%d" % d],
+                srcs=[T.SA[:, 96 * (d - 1):96 * d]], dsts=[T["RW%d" % d][:, 0:96]]))
+            total["ls"] += len(es)
+            total["rt%d" % d] = len(topo.engines(cores[(rank + d) % N], core)[cuts[i]:cuts[i + 1]])
+            note((None, "rt%d" % d, total["rt%d" % d]), [], ["RV%d" % d])
+        g.remote_dma_fused(trs, local_sem=T.sem.ls)
+
+    for f in (last_1, last_2, last_3, last_4):
+        f(0)
+        f(1)
+    rows(0)
+    rows(1)
+    for f in (last_1, last_2, last_3, last_4):
+        f(2)
+    rows(2)
+    send((1, 2, 3, 4), ["SA0", "SA1"], (0, 4, 8, 12, 16))
+    send((5, 6, 7), ["SA2"], (0, 4, 8, 16))
+    for k in (0, 1):
+        ts([POS[k]], ["Q1_%d" % k], cols("Q1", k), T[POS[k]][:, 0:64], -96.0, None, ALU.add)
     ts(["CJ"], ["JT"], T.JT[:], T.CJ[:, 0:16], -1.0, -1.0, ALU.mult, ALU.add)
-    tt(["Q1", "HB"], ["GQ"], T.GQ[:, 16:128], T.Q1[:, 16:128], T.HB[:, 16:128], ALU.mult)
-    op("V", v.tensor_tensor, ["JT", "HB"], ["GQ"], T.GQ[:, 0:16], T.JT[:], T.HB[:, 0:16], ALU.mult, add=True)
-    op("V", v.transpose, ["GQ"], ["GX"], T.GX[:], T.GQ[:])
-    exchange("GX", 4)
-    op("V", v.transpose, ["EX"], ["GT"], T.GT[:], T.EX[:, 0:128])
+    tt(["Q1_0", "Q1_1", "HB0", "HB1"], ["GQ"], T.GQ[:, 16:128], T.Q1[:, 16:128], T.HB[:, 16:128], ALU.mult)
+    op("V", v.tensor_tensor, ["JT", "HB0"], ["GQ"], T.GQ[:, 0:16], T.JT[:], T.HB[:, 0:16], ALU.mult, add=True)
+    turn("GQ", "GX", T.GX[:], T.GQ[:])
+    exchange(("GX", "GX"), "EX", 0, 4)
+    turn("EX", "GT", T.GT[:], T.EX[:, 0:128])
     ts(["GT"], ["GO0"], T.GO[:, 0:16], T.GT[:, 0:16], 256.0, None, ALU.add)
     ts(["GT"], ["GO1"], T.GO[:, 16:128], T.GT[:, 16:128], 96.0, None, ALU.add)
 
     def sums_of(d):
         return T["RW%d" % d][:].indirect(T.GO[:, d * 16:d * 16 + 16]), ["RV%d" % d, "RZ%d" % d, "GO%d" % min(d, 1)]
 
+    def plus(d, x, y):
+        win, rs = sums_of(d)
+        tt(rs + [x], [y], T[y][:], win, T[x][:], ALU.add)
+
     for d in range(3):
         win, rs = sums_of(d)
         act(rs, ["A%d" % d], T["A%d" % d][:], win, COPY)
-    for d, x, y in ((3, "A0", "Y0"), (4, "A1", "Y1"), (5, "A2", "Y2"), (6, "Y0", "A0"), (7, "Y1", "A1")):
-        win, rs = sums_of(d)
-        tt(rs + [x], [y], T[y][:], win, T[x][:], ALU.add)
-    tt(["A0", "Y2"], ["Y0"], T.Y0[:], T.A0[:], T.Y2[:], ALU.add)
-    tt(["Y0", "A1"], ["Y1"], T.Y1[:], T.Y0[:], T.A1[:], ALU.add)
-    dma("S", "dY", T.y[:, :], T.Y1[0::16, :], ["Y1"], ["y"])
+    plus(3, "A0", "Y0")
+    plus(4, "A1", "Y1")
+    tt(["Y0", "A2"], ["Y2"], T.Y2[:], T.Y0[:], T.A2[:], ALU.add)
+    tt(["Y1", "Y2"], ["Y3"], T.Y3[:], T.Y1[:], T.Y2[:], ALU.add)
+    plus(5, "Y3", "Y0")
+    plus(6, "Y0", "Y1")
+    plus(7, "Y1", "Y2")
+    dma("S", "dY", T.y[:, :], T.Y2[0::16, :], ["Y2"], ["y"])
     for sem in sorted(total):
         if max([seen.get((q, sem), 0) for q in queue]) < total[sem]:
             g.wait_ge(T.sem[sem], total[sem])

@@ -89,11 +89,11 @@ def rank_program(g, core, T, topo):
         method(*args, **kw).then_inc(T.sem[sem], 1)
         note(h, reads, writes, add)
 
-    def dma(q, sem, out, in_, reads, writes, add=False):
+    def dma(q, sem, out, in_, reads, writes):
         deps(q, reads, writes)
         total[sem] = total.get(sem, 0) + 16
         queue[q].dma_start(out, in_).then_inc(T.sem[sem], 16)
-        note((None, sem, total[sem]), reads, writes, add)
+        note((None, sem, total[sem]), reads, writes)
 
     v, a, p = g.vector, g.scalar, g.tensor
 
@@ -119,11 +119,11 @@ def rank_program(g, core, T, topo):
         op("A", a.activation, reads, writes, out, in_, func, **kw)
 
     dma("S", "dN0", T.N0[:], T.nodes[:, 0:8], [], ["N0"])
-    fill("Pi", T.Pi[:], 0)
+    fill("Pz", T.Pi[:], 0)
     op("G", g.iota, [], ["IK"], T.IK[:], [[1, 1]], 0, 1)
     op("G", g.iota, [], ["IRf"], T.IRf[:], [[1, 128]], 0, 0, allow_small_or_imprecise_dtypes=True)
     for i in range(6):
-        dma("S" if i < 3 else "A", "dP", T.Pi[i::16, :], T.pts[i % 3::3, :], [], ["Pi"], add=True)
+        dma("S" if i < 3 else "A", "dP", T.Pi[i::16, :], T.pts[i % 3::3, :], ["Pz"], ["Pi%d" % i])
     dma("S", "dSW", T.SKi[:], T.nodes[6::16, :], [], ["SKi"])
     dma("A", "dSW", T.Wi[:], T.nodes[7::16, :], [], ["Wi"])
     dsts = [cores[(rank + e) % N] for e in range(1, N)]
@@ -170,11 +170,11 @@ def rank_program(g, core, T, topo):
     fill("ONE", T.ONE[:], 1.0)
     tt(["BASE", "PEN0"], ["TG0"], T.TG0[:], T.BASE[:], T.PEN0[:], ALU.add)
     tt(["BASE", "PEN1"], ["TG1"], T.TG1[:], T.BASE[:], T.PEN1[:], ALU.add)
-    ts(["Pi", "SG"], ["PL0"], T.PL[:, 0:256], T.Pi[:], T.SG[:, 0:1], None, ALU.mult)
     for x in (0, 1):
         for y in (0, 1):
             n = "L%d%d" % (x, y)
             ts(["IRf", "TG%d" % x], [n], T[n][:], T.IRf[:], float(-y), T["TG%d" % x][:, 0:1], ALU.add, ALU.is_equal)
+    ts(["Pi%d" % i for i in range(6)] + ["SG"], ["PL0"], T.PL[:, 0:256], T.Pi[:], T.SG[:, 0:1], None, ALU.mult)
     vc(["SKi"], ["SKh"], T.SKh[:], T.SKi[:])
     ts(["Wi"], ["Wb"], T.Wb[:], T.Wi[:], 65536.0, None, ALU.add)
     fill("C1", T.C1[:], 0.0)
@@ -182,25 +182,20 @@ def rank_program(g, core, T, topo):
     tt(["SKi", "SKh"], ["SKl"], T.SKl[:], T.SKi[:], T.SKh[:], ALU.subtract)
     fill("C2", T.C2[:], 0.0)
     tt(["Wb", "Wh"], ["Wl"], T.Wl[:], T.Wb[:], T.Wh[:], ALU.subtract)
-    wr["AX"] = []
     for i, n in enumerate(("SKh", "SKl", "Wh", "Wl")):
-        dma("S", "dAX", T.AX[i::16, 0:M], T[n][:], [n, "AXm"], ["AX"], add=True)
-    ts(["AF"], ["W1"], T.W1[:], T.AF[:], 1.5, None, ALU.is_gt)
-    ts(["AF"], ["W2"], T.W2[:], T.AF[:], 3.5, None, ALU.is_lt)
-    ts(["AF"], ["V4"], T.V4[:], T.AF[:], 4.0, None, ALU.is_equal)
-    ts(["AF"], ["V1"], T.V1[:], T.AF[:], 1.5, None, ALU.is_lt)
-    tt(["W1", "W2"], ["W3"], T.W3[:], T.W1[:], T.W2[:], ALU.mult)
+        dma("S", "dAX", T.AX[i::16, 0:M], T[n][:], [n, "AXm"], ["AX%d" % i])
     fill("AXs", T.AX[:, M:MW], 1024.0)
-    wr["AX"] = wr["AX"] + wr["AXm"] + wr["AXs"]
-    await_("V", wr["C1"] + wr["C2"])
-    for (n, q, col, f) in (("C1", 0, "VM", 4096.0), ("C1", 1, "VM", -2048.0), ("C1", 3, "VM", -2048.0),
-                           ("C2", 0, "V4", 2.0 ** -16), ("C2", 1, "W3", 2.0 ** -6), ("C2", 2, "V1", 1.0),
-                           ("C2", 3, "V4", 2.0 ** -6)):
-        ts(["G8", col], [n], T[n][:, q::4], T.G8[:], T[col][:, 0:1], f, ALU.mult, ALU.mult)
-    fill("TWs", T.TW[:, M:MW], 4194304.0)
+    AX = ["AXm", "AXs"] + ["AX%d" % i for i in range(4)]
     act(["TWa", "SG"], ["TWa"], T.TW[:, 0:1024], T.TW[:, 0:1024], COPY, scale=T.SG[:, 0:1])
     act(["TWb", "SG"], ["TWb"], T.TW[:, 1024:M], T.TW[:, 1024:M], COPY, scale=T.SG[:, 0:1])
     TW = ["TWa", "TWb", "TWs"]
+
+    def coefficients():
+        await_("V", wr["C1"] + wr["C2"])
+        for (n, q, col, f) in (("C1", 0, "VM", 4096.0), ("C1", 1, "VM", -2048.0), ("C1", 3, "VM", -2048.0),
+                               ("C2", 0, "V4", 2.0 ** -16), ("C2", 1, "W3", 2.0 ** -6), ("C2", 2, "V1", 1.0),
+                               ("C2", 3, "V4", 2.0 ** -6)):
+            ts(["G8", col], [n], T[n][:, q::4], T.G8[:], T[col][:, 0:1], f, ALU.mult, ALU.mult)
 
     COUNT, POS, EXCH = ["PF", "AC"], ["PR", "PQ"], ["EX", "PS0"]
 
@@ -264,8 +259,9 @@ def rank_program(g, core, T, topo):
         fill("RZ%d" % d, T["RW%d" % d][:, (256 if d == 0 else 96):(288 if d == 0 else 128)], 0.0)
 
     ts(["N0", "SG"], ["BX0"], T.BX[:, 0:1], T.N0[:, 0:1], T.SG[:, 0:1], None, ALU.mult)
+    inside_0 = len(wr)
     ts(["BXi", "SG"], ["BX1"], T.BX[:, 1:8], T.BXi[:, 1:8], T.SG[:, 0:1], None, ALU.mult)
-    for d in (1, 2, 3, 0, 4):
+    for d in (0, 1, 2, 3, 4):
         inside(d)
     hits(0)
     inside(5)
@@ -281,23 +277,26 @@ def rank_program(g, core, T, topo):
     back(0)
     place(1)
     list_(0)
-    fill("PS1", T.PS1[:, 0:96], 0.0)
+    ts(["AF"], ["W1"], T.W1[:], T.AF[:], 1.5, None, ALU.is_gt)
     swap(1)
     scatter(1)
     back(1)
-    scatter(2)
+    ts(["AF"], ["W2"], T.W2[:], T.AF[:], 3.5, None, ALU.is_lt)
     list_(1)
-    scatter(3)
-    for d in range(4, 8):
+    for d in range(2, 8):
         scatter(d)
-        if d == 4:
-            ts(["AX", "IRf"], ["AX0"], T.AX0[:], T.IRf[:], 0.0, T.AX[:, 0:1], ALU.mult, ALU.add)
-            fill("PS0", T.PS0[:, 0:96], 0.0)
-            fill("PS2", T.PS2[:, 0:96], 0.0)
-            ts(["IRf", "KF"], ["IDf"], T.IDf[:], T.IRf[:], T.KF[:, 0:1], None, ALU.is_equal)
-            for b in "012":
-                fill("OF" + b, T["OF" + b][:], 1)
-                ts(["IRf"], ["NX" + b], T["NX" + b][:], T.IRf[:, 0:32], 0.0, 1.0, ALU.mult, ALU.add)
+    ts(["AF"], ["V4"], T.V4[:], T.AF[:], 4.0, None, ALU.is_equal)
+    ts(["AF"], ["V1"], T.V1[:], T.AF[:], 1.5, None, ALU.is_lt)
+    tt(["W1", "W2"], ["W3"], T.W3[:], T.W1[:], T.W2[:], ALU.mult)
+    ts(AX + ["IRf"], ["AX0"], T.AX0[:], T.IRf[:], 0.0, T.AX[:, 0:1], ALU.mult, ALU.add)
+    for b in "012":
+        fill("OF" + b, T["OF" + b][:], 1)
+        fill("PS" + b, T["PS" + b][:, 0:96], 0.0)
+    fill("TWs", T.TW[:, M:MW], 4194304.0)
+    coefficients()
+    for b in "012":
+        ts(["IRf"], ["NX" + b], T["NX" + b][:], T.IRf[:, 0:32], 0.0, 1.0, ALU.mult, ALU.add)
+    ts(["IRf", "KF"], ["IDf"], T.IDf[:], T.IRf[:], T.KF[:, 0:1], None, ALU.is_equal)
 
     def blocks(b):
         n = BATCH[b][1]
@@ -315,7 +314,7 @@ def rank_program(g, core, T, topo):
             ts(rs, ws, out, pt, T.TW[:, 1:2], None, ALU.is_lt)
         else:
             tt(rs + ["OF%d" % b], ws, out, T.TW[:].indirect(offs), pt, ALU.is_gt)
-        act(["AX", "OF%d" % b], ["D2_%d" % b], T["D2_%d" % b][:, 0:n], T.AX[:].indirect(offs), COPY)
+        act(AX + ["OF%d" % b], ["D2_%d" % b], T["D2_%d" % b][:, 0:n], T.AX[:].indirect(offs), COPY)
         for (j, x, y) in blocks(b):
             out = T["PS%d" % b][0:y - x, j * 32:j * 32 + 32]
             mm(["D2_%d" % b, "C2"], ["PS%d" % b], out, T["D2_%d" % b][:, x:y], T.C2[:], True, False)
@@ -324,14 +323,38 @@ def rank_program(g, core, T, topo):
     def weigh(b):
         act(["PS%d" % b], ["ZZ%d" % b], T.ZZ[:, b * 48:b * 48 + 48], T["PS%d" % b][:, 1:96:2], RELU)
 
-    def add_up(t):
-        mm(["ZZ0", "ZZ1", "ZZ2", "IDf"], ["AC"], T.AC[:, 0:144], T.IDf[:], T.ZZ[:], t == 0, t == STEPS - 1)
+    def add_up(b, t):
+        if b == 1:
+            mm(["ZZ0", "ZZ1", "IDf"], ["AC"], T.AC[:, 0:96], T.IDf[:], T.ZZ[:, 0:96], t == 0, t == STEPS - 1)
+        if b == 2:
+            mm(["ZZ2", "IDf"], ["PF"], T.PF[:, 0:48], T.IDf[:], T.ZZ[:, 96:144], t == 0, t == STEPS - 1)
+
+    def list_work(s):
+        if s == 0:
+            for k in (0, 1):
+                ts([POS[k]], ["Q1_%d" % k], cols("Q1", k), T[POS[k]][:, 0:64], -96.0, None, ALU.add)
+            ts(["CJ"], ["JT"], T.JT[:], T.CJ[:, 0:16], -1.0, -1.0, ALU.mult, ALU.add)
+            fill("F0z", T.F0[:, 0:1152], 0.0)
+        if s == 1:
+            tt(["Q1_0", "Q1_1", "HB0", "HB1"], ["GQ"], T.GQ[:, 16:128], T.Q1[:, 16:128], T.HB[:, 16:128], ALU.mult)
+            op("V", v.tensor_tensor, ["JT", "HB0"], ["GQ"], T.GQ[:, 0:16], T.JT[:], T.HB[:, 0:16], ALU.mult, add=True)
+            vc(["F0z"], ["HITz"], T.HIT[:], T.F0[:, 0:1152])
+        if s == 2:
+            turn("GQ", "GX", T.GX[:], T.GQ[:])
+            exchange(("GX", "GX"), "PR", 0, 4)
+            vc(["F0z"], ["LOTz"], T.LOT[:], T.F0[:, 0:1152])
+        if s == 4:
+            turn("PR", "GT", T.GT[:], T.PR[:, 0:128])
+        if s == 5:
+            ts(["GT"], ["GO0"], T.GO[:, 0:16], T.GT[:, 0:16], 256.0, None, ALU.add)
+            ts(["GT"], ["GO1"], T.GO[:, 16:128], T.GT[:, 16:128], 96.0, None, ALU.add)
+            ts(["IRf", "KF"], ["IDh"], T.IDh[:], T.IRf[:], T.KF[:, 0:1], None, ALU.is_equal)
 
     for b in range(3):
         for (j, x, y) in blocks(b):
             mm(["AX0", "C2"], ["PS%d" % b], T["PS%d" % b][0:y - x, j * 32:j * 32 + 32], T.AX0[:, 0:y - x], T.C2[:], True, True)
         weigh(b)
-    add_up(0)
+        add_up(b, 0)
     for s in range(3 * STEPS):
         t, b = s // 3 + 1, s % 3
         t1, b1 = (s - 1) // 3 + 1, (s - 1) % 3
@@ -347,25 +370,21 @@ def rank_program(g, core, T, topo):
             tt([ps, tmp], [nx], T[nx][:, 0:24], T[ps][:, 2:96:4], T[tmp][:], ALU.min)
         if go2:
             vc(["WT%d" % b2], ["OF%d" % b2], T["OF%d" % b2][:], T["WT%d" % b2][:])
+            weigh(b2)
         if go1:
             turn(nx, xt, T[xt][:], T[nx][:])
             exchange((xt, xt), "EX", 0, 1)
-        if s >= 1:
+        if go2:
+            add_up(b2, t2)
+        if s >= 1 and t1 == STEPS:
             weigh(b1)
-        if b1 == 2 and s >= 1 and t1 < STEPS:
-            add_up(t1)
-        if s == 0:
-            fill("F0z", T.F0[:, 0:1152], 0.0)
-            ts(["IRf", "KF"], ["IDh"], T.IDh[:], T.IRf[:], T.KF[:, 0:1], None, ALU.is_equal)
-        if s == 1:
-            vc(["F0z"], ["HITz"], T.HIT[:], T.F0[:, 0:1152])
-        if s == 2:
-            vc(["F0z"], ["LOTz"], T.LOT[:], T.F0[:, 0:1152])
+        list_work(s)
     weigh(2)
 
     def last_1(b):
         x = slice(b * 48, b * 48 + 48)
-        tt(["AC", "ZZ%d" % b], ["EE%d" % b], T.EE[:, x], T.AC[:, x], T.ZZ[:, x], ALU.add)
+        acc = T.AC[:, x] if b < 2 else T.PF[:, 0:48]
+        tt(["AC" if b < 2 else "PF", "ZZ%d" % b], ["EE%d" % b], T.EE[:, x], acc, T.ZZ[:, x], ALU.add)
 
     def last_2(b):
         tt(["EE%d" % b], ["SS%d" % b], T.SS[:, b * 24:b * 24 + 24], T.EE[:, b * 48:b * 48 + 48:2],
@@ -416,16 +435,6 @@ def rank_program(g, core, T, topo):
     rows(2)
     send((1, 2, 3, 4), ["SA0", "SA1"], (0, 4, 8, 12, 16))
     send((5, 6, 7), ["SA2"], (0, 4, 8, 16))
-    for k in (0, 1):
-        ts([POS[k]], ["Q1_%d" % k], cols("Q1", k), T[POS[k]][:, 0:64], -96.0, None, ALU.add)
-    ts(["CJ"], ["JT"], T.JT[:], T.CJ[:, 0:16], -1.0, -1.0, ALU.mult, ALU.add)
-    tt(["Q1_0", "Q1_1", "HB0", "HB1"], ["GQ"], T.GQ[:, 16:128], T.Q1[:, 16:128], T.HB[:, 16:128], ALU.mult)
-    op("V", v.tensor_tensor, ["JT", "HB0"], ["GQ"], T.GQ[:, 0:16], T.JT[:], T.HB[:, 0:16], ALU.mult, add=True)
-    turn("GQ", "GX", T.GX[:], T.GQ[:])
-    exchange(("GX", "GX"), "EX", 0, 4)
-    turn("EX", "GT", T.GT[:], T.EX[:, 0:128])
-    ts(["GT"], ["GO0"], T.GO[:, 0:16], T.GT[:, 0:16], 256.0, None, ALU.add)
-    ts(["GT"], ["GO1"], T.GO[:, 16:128], T.GT[:, 16:128], 96.0, None, ALU.add)
 
     def sums_of(d):
         return T["RW%d" % d][:].indirect(T.GO[:, d * 16:d * 16 + 16]), ["RV%d" % d, "RZ%d" % d, "GO%d" % min(d, 1)]

from concourse.bass import DstId, RemoteDMATransfer
from concourse.mybir import AluOpType, ActivationFunctionType

N = 8
M = 2048
MW = 2056
STEPS = 14
BATCH = [(0, 320), (320, 320), (640, 288)]
ALU = AluOpType
COPY = ActivationFunctionType.Copy
RELU = ActivationFunctionType.Relu

SCRATCH = {}
for _n, _w, _t in (
        [(n, 1, "float32") for n in ("KF AF U2 V32 UV BASE PEN0 PEN1 TG0 TG1 R1 R2 R3 SG P16 VM V4 V1 W1 W2 W3").split()]
        + [(n, 1, "int32") for n in "IK AI UI VI BI GI HI16".split()]
        + [(n, 128, "int32") for n in "SKi Wi".split()]
        + [(n, 128, "float32") for n in "CJ IRf IDf Wb MS ST Q1 GT".split()]
        + [(n, 128, "bfloat16") for n in "TRI ONE AX0 SKh SKl Wh Wl HB NB".split()]
        + [(n, 128, "float16") for n in "IDh L00 L01 L10 L11 SC SX GQ GX".split()]
        + [(n, 256, "float32") for n in "A0 A1 A2 Y0 Y1 Y2 Y3".split()]
        + [("SO", 128, "uint16"), ("GO", 128, "uint16"), ("G8", 8, "float32"), ("CM", 8, "bfloat16"),
           ("C1", 32, "bfloat16"), ("C2", 32, "bfloat16"), ("JT", 16, "float32"), ("N0", 8, "int32"),
           ("BXi", 8, "int32"), ("BX", 8, "float32"), ("Pi", 256, "int32"), ("PL", 928, "float32"),
           ("TW", MW, "float32"), ("AX", MW, "bfloat16"), ("F0", 2048, "bfloat16"), ("CP", 7 * 256, "float32"),
           ("HIT", 1152, "float16"), ("LOT", 1152, "float16"), ("EE", 144, "float32"), ("SS", 72, "float32"),
           ("SA", 672, "float32"), ("ZZ", 144, "float32"), ("RW0", 288, "float32")]
        + [("RW%d" % d, 128, "float32") for d in range(1, 8)]):
    SCRATCH[_n] = ("sbuf", [128, _w], _t)
for _b in range(3):
    for _n, _w, _t in (("D1_", 320, "bfloat16"), ("D2_", 320, "bfloat16"), ("OF", 32, "uint16"), ("NX", 32, "float16"),
                       ("TT", 24, "float32"), ("XT", 32, "float16"), ("WT", 32, "float32")):
        SCRATCH["%s%d" % (_n, _b)] = ("sbuf", [128, _w], _t)
PSUM = ["PF", "PR", "PQ", "PS0", "PS1", "PS2", "EX", "AC"]
for _n in PSUM:
    SCRATCH[_n] = ("psum", [128, 512], "float32")

DMASEMS = ["dN0", "dP", "dSW", "dT0", "dT1", "dAX", "dY"]
SEMAPHORES = (["cV", "cA", "cP", "cG", "box", "ls"] + DMASEMS
              + ["pt%d" % d for d in range(1, 8)] + ["rt%d" % d for d in range(1, 8)])


def rank_program(g, core, T, topo):
    rank = T.rank_of(core)
    if rank is None:
        return
    cores = T.cores
    queue = {"V": g.vector, "A": g.scalar, "P": g.tensor, "G": g, "S": g.sync}
    total = {"ls": 0}
    seen = {}
    wr, rd = {}, {}

    def await_(q, handles):
        need = {}
        for (_, sem, val) in handles:
            if sem in DMASEMS:
                val = total[sem]
            need[sem] = max(need.get(sem, 0), val)
        for sem in sorted(need):
            if seen.get((q, sem), 0) < need[sem]:
                queue[q].wait_ge(T.sem[sem], need[sem])
                seen[(q, sem)] = need[sem]

    def deps(q, reads, writes):
        hs = []
        for t in reads:
            hs += wr.get(t, [])
            if t in PSUM:
                hs += [h for h in rd.get(t, []) if h[0] != q]
        for t in writes:
            hs += [h for h in wr.get(t, []) + rd.get(t, []) if h[0] != q]
        await_(q, hs)

    def note(h, reads, writes, add=False):
        for t in reads:
            rd.setdefault(t, []).append(h)
        for t in writes:
            if add:
                wr.setdefault(t, []).append(h)
            else:
                wr[t] = [h]
                rd[t] = []

    def op(q, method, reads, writes, *args, add=False, **kw):
        deps(q, reads, writes)
        sem = "c" + q
        total[sem] = total.get(sem, 0) + 1
        h = (q, sem, total[sem])
        method(*args, **kw).then_inc(T.sem[sem], 1)
        note(h, reads, writes, add)

    def dma(q, sem, out, in_, reads, writes):
        deps(q, reads, writes)
        total[sem] = total.get(sem, 0) + 16
        queue[q].dma_start(out, in_).then_inc(T.sem[sem], 16)
        note((None, sem, total[sem]), reads, writes)

    v, a, p = g.vector, g.scalar, g.tensor

    def ts(reads, writes, out, in0, s1, s2, *ops):
        op("V", v.tensor_scalar, reads, writes, out, in0, s1, s2, *ops)

    def tt(reads, writes, out, in0, in1, o):
        op("V", v.tensor_tensor, reads, writes, out, in0, in1, o)

    def vc(reads, writes, out, in_):
        op("V", v.tensor_copy, reads, writes, out, in_)

    def turn(x, y, out, in_):
        op("V", v.transpose, [x], [y], out, in_)

    def fill(tag, ap, c):
        op("V", v.memset, [], [tag], ap, c)

    def mm(reads, writes, out, lhsT, rhs, start, stop):
        op("P", p.matmul, reads, writes, out, lhsT, rhs, start, stop)

    def act(reads, writes, out, in_, func, **kw):
        op("A", a.activation, reads, writes, out, in_, func, **kw)

    dma("S", "dN0", T.N0[:], T.nodes[:, 0:8], [], ["N0"])
    fill("Pz", T.Pi[:], 0)
    op("G", g.iota, [], ["IK"], T.IK[:], [[1, 1]], 0, 1)
    op("G", g.iota, [], ["IRf"], T.IRf[:], [[1, 128]], 0, 0, allow_small_or_imprecise_dtypes=True)
    for i in range(6):
        dma("S" if i < 3 else "A", "dP", T.Pi[i::16, :], T.pts[i % 3::3, :], ["Pz"], ["Pi%d" % i])
    dma("S", "dSW", T.SKi[:], T.nodes[6::16, :], [], ["SKi"])
    dma("A", "dSW", T.Wi[:], T.nodes[7::16, :], [], ["Wi"])
    dsts = [cores[(rank + e) % N] for e in range(1, N)]
    deps("G", ["N0"], [])
    ids = []
    for dcore in dsts:
        rid, pid, _ = topo.addr(dcore)
        ids.append(DstId(rid=rid, pnc=pid))
    lanes = len(topo.engines(core, dsts[0]))
    total["ls"] += lanes
    g.remote_dma_fused([RemoteDMATransfer(
        dst_ids=ids, dma_engine_mask=topo.mask(core, dsts[0]), remote_sem=T.sem.box, srcs=[T.N0[:, 0:1]],
        dsts=[T.BXi[:, N - e:N - e + 1] for e in range(1, N)])], local_sem=T.sem.ls)
    total["box"] = (N - 1) * lanes
    note((None, "box", total["box"]), [], ["BXi"])
    dma("G", "dT0", T.TW[:, 0:1024], T.nodes[:, 0:1024], [], ["TWa"])
    dma("G", "dT1", T.TW[:, 1024:2048], T.nodes[:, 1024:2048], [], ["TWb"])
    op("G", g.iota, [], ["CJ"], T.CJ[:], [[0, 8], [-128, 2], [0, 8]], 255, -1, allow_small_or_imprecise_dtypes=True)
    op("G", g.iota, [], ["AXm"], T.AX[:, 0:M], [[0, M]], 65536, 0, allow_small_or_imprecise_dtypes=True)

    ts(["IK"], ["AI"], T.AI[:], T.IK[:], 15, None, ALU.bitwise_and)
    vc(["IK"], ["KF"], T.KF[:], T.IK[:])
    ts(["IK"], ["HI16"], T.HI16[:], T.IK[:], 4, None, ALU.logical_shift_right)
    vc(["AI"], ["AF"], T.AF[:], T.AI[:])
    ts(["IK"], ["UI"], T.UI[:], T.IK[:], 5, None, ALU.logical_shift_right)
    vc(["HI16"], ["P16"], T.P16[:], T.HI16[:])
    ts(["AF"], ["R1"], T.R1[:], T.AF[:], 2.5, None, ALU.is_gt)
    ts(["AF"], ["R2"], T.R2[:], T.AF[:], 5.5, -2.0, ALU.is_lt, ALU.mult)
    ts(["IRf", "P16"], ["G8"], T.G8[:], T.IRf[:, 0:8], T.P16[:, 0:1], None, ALU.is_equal)
    ts(["AF"], ["VM"], T.VM[:], T.AF[:], 5.5, None, ALU.is_lt)
    tt(["R1", "R2"], ["R3"], T.R3[:], T.R1[:], T.R2[:], ALU.mult)
    ts(["IK"], ["VI"], T.VI[:], T.IK[:], 1, 3, ALU.logical_shift_right, ALU.bitwise_and)
    ts(["IK"], ["BI"], T.BI[:], T.IK[:], 24, None, ALU.bitwise_and)
    ts(["R3"], ["SG"], T.SG[:], T.R3[:], 1.0, None, ALU.add)
    ts(["IK"], ["GI"], T.GI[:], T.IK[:], 1, None, ALU.bitwise_and)
    ts(["G8", "VM"], ["CM"], T.CM[:], T.G8[:], T.VM[:, 0:1], None, ALU.mult)
    ts(["UI"], ["U2"], T.U2[:], T.UI[:], 2.0, None, ALU.mult)
    ts(["VI"], ["V32"], T.V32[:], T.VI[:], 32.0, None, ALU.mult)
    ts(["GI"], ["PEN0"], T.PEN0[:], T.GI[:], 1000.0, None, ALU.mult)
    ts(["GI"], ["PEN1"], T.PEN1[:], T.GI[:], -1000.0, 1000.0, ALU.mult, ALU.add)
    tt(["U2", "V32"], ["UV"], T.UV[:], T.U2[:], T.V32[:], ALU.add)
    ts(["IRf", "KF"], ["TRI"], T.TRI[:], T.IRf[:], T.KF[:, 0:1], None, ALU.is_gt)
    tt(["UV", "BI"], ["BASE"], T.BASE[:], T.UV[:], T.BI[:], ALU.add)
    fill("ONE", T.ONE[:], 1.0)
    tt(["BASE", "PEN0"], ["TG0"], T.TG0[:], T.BASE[:], T.PEN0[:], ALU.add)
    tt(["BASE", "PEN1"], ["TG1"], T.TG1[:], T.BASE[:], T.PEN1[:], ALU.add)
    for x in (0, 1):
        for y in (0, 1):
            n = "L%d%d" % (x, y)
            ts(["IRf", "TG%d" % x], [n], T[n][:], T.IRf[:], float(-y), T["TG%d" % x][:, 0:1], ALU.add, ALU.is_equal)
    ts(["Pi%d" % i for i in range(6)] + ["SG"], ["PL0"], T.PL[:, 0:256], T.Pi[:], T.SG[:, 0:1], None, ALU.mult)
    vc(["SKi"], ["SKh"], T.SKh[:], T.SKi[:])
    ts(["Wi"], ["Wb"], T.Wb[:], T.Wi[:], 65536.0, None, ALU.add)
    fill("C1", T.C1[:], 0.0)
    vc(["Wb"], ["Wh"], T.Wh[:], T.Wb[:])
    tt(["SKi", "SKh"], ["SKl"], T.SKl[:], T.SKi[:], T.SKh[:], ALU.subtract)
    fill("C2", T.C2[:], 0.0)
    tt(["Wb", "Wh"], ["Wl"], T.Wl[:], T.Wb[:], T.Wh[:], ALU.subtract)
    for i, n in enumerate(("SKh", "SKl", "Wh", "Wl")):
        dma("S", "dAX", T.AX[i::16, 0:M], T[n][:], [n, "AXm"], ["AX%d" % i])
    fill("AXs", T.AX[:, M:MW], 1024.0)
    AX = ["AXm", "AXs"] + ["AX%d" % i for i in range(4)]
    act(["TWa", "SG"], ["TWa"], T.TW[:, 0:1024], T.TW[:, 0:1024], COPY, scale=T.SG[:, 0:1])
    act(["TWb", "SG"], ["TWb"], T.TW[:, 1024:M], T.TW[:, 1024:M], COPY, scale=T.SG[:, 0:1])
    TW = ["TWa", "TWb", "TWs"]

    def coefficients():
        await_("V", wr["C1"] + wr["C2"])
        for (n, q, col, f) in (("C1", 0, "VM", 4096.0), ("C1", 1, "VM", -2048.0), ("C1", 3, "VM", -2048.0),
                               ("C2", 0, "V4", 2.0 ** -16), ("C2", 1, "W3", 2.0 ** -6), ("C2", 2, "V1", 1.0),
                               ("C2", 3, "V4", 2.0 ** -6)):
            ts(["G8", col], [n], T[n][:, q::4], T.G8[:], T[col][:, 0:1], f, ALU.mult, ALU.mult)

    COUNT, POS, EXCH = ["PF", "AC"], ["PR", "PQ"], ["EX", "PS0"]

    def inside(d):
        ts(["PL0", "BX%d" % min(d, 1)], ["F0_%d" % d], T.F0[:, d * 256:d * 256 + 256], T.PL[:, 0:256], T.BX[:, d:d + 1], None, ALU.is_lt)
        ps = COUNT[d // 4]
        for jb in (0, 1):
            c = d * 16 + jb * 8
            mm(["F0_%d" % d, "CM"], [ps], T[ps][:, c % 64:c % 64 + 8],
               T.F0[:, d * 256 + jb * 128:d * 256 + jb * 128 + 128], T.CM[:], True, True)

    def cols(n, k):
        return T[n][:, 64 * k:64 * k + 64]

    def hits(k):
        ts([COUNT[k]], ["HB%d" % k], cols("HB", k), T[COUNT[k]][:, 0:64], 0.5, None, ALU.is_lt)
        ts([COUNT[k]], ["NB%d" % k], cols("NB", k), T[COUNT[k]][:, 0:64], 0.5, None, ALU.is_gt)
        ps = POS[k]
        mm(["HB%d" % k, "TRI"], [ps], T[ps][:, 0:64], T.TRI[:], cols("HB", k), True, False)
        for d in range(4):
            mm(["HB%d" % k, "ONE"], [ps], T[ps][:, d * 16 + 8:d * 16 + 16], T.ONE[:],
               T.HB[:, k * 64 + d * 16:k * 64 + d * 16 + 8], False, d == 3)

    def away(k):
        tt(["NB%d" % k, "CJ"], ["MS%d" % k], cols("MS", k), cols("NB", k), cols("CJ", k), ALU.mult)

    def place(k):
        tt([POS[k], "MS%d" % k], ["SC%d" % k], cols("SC", k), T[POS[k]][:, 0:64], cols("MS", k), ALU.add)

    def exchange(x, ps, c, n):
        tag, buf = x
        for b in range(n):
            for g0 in (0, 1):
                for p4 in (0, 1):
                    m = "L%d%d" % (g0, p4)
                    mm([tag, m], [ps], T[ps][:, b * 32 + g0 * 16:b * 32 + g0 * 16 + 16], T[m][:],
                       T[buf][:, c + b * 32 + p4 * 16:c + b * 32 + p4 * 16 + 16], p4 == 0, p4 == 1)

    def swap(k):
        turn("SC%d" % k, "SX%d" % k, cols("SX", k), cols("SC", k))
        exchange(("SX%d" % k, "SX"), EXCH[k], 64 * k, 2)

    def back(k):
        turn(EXCH[k], "ST%d" % k, cols("ST", k), T[EXCH[k]][:, 0:64])

    def list_(k):
        vc(["ST%d" % k], ["SO%d" % k], cols("SO", k), cols("ST", k))

    def scatter(d):
        vc(["PL0", "SO%d" % (d // 4)], ["CP%d" % d], T.CP[:, (d - 1) * 256:d * 256].indirect(T.SO[:, d * 16:d * 16 + 16]), T.PL[:, 0:256])
        deps("G", ["CP%d" % d] + ["RZ%d" % k for k in range(8)], [])
        dst = cores[(rank + d) % N]
        rid, pid, _ = topo.addr(dst)
        total["ls"] += len(topo.engines(core, dst))
        g.remote_dma(T.PL[:, 256 + 96 * (d - 1):256 + 96 * d], T.CP[:, (d - 1) * 256:(d - 1) * 256 + 96],
                     T.sem["pt%d" % d], T.sem.ls, pid, rid, topo.mask(core, dst))
        total["pt%d" % d] = len(topo.engines(cores[(rank - d) % N], core))
        note((None, "pt%d" % d, total["pt%d" % d]), [], ["PL%d" % d])

    def zero_slot(d):
        fill("RZ%d" % d, T["RW%d" % d][:, (256 if d == 0 else 96):(288 if d == 0 else 128)], 0.0)

    ts(["N0", "SG"], ["BX0"], T.BX[:, 0:1], T.N0[:, 0:1], T.SG[:, 0:1], None, ALU.mult)
    inside_0 = len(wr)
    ts(["BXi", "SG"], ["BX1"], T.BX[:, 1:8], T.BXi[:, 1:8], T.SG[:, 0:1], None, ALU.mult)
    for d in (0, 1, 2, 3, 4):
        inside(d)
    hits(0)
    inside(5)
    away(0)
    inside(6)
    place(0)
    inside(7)
    swap(0)
    hits(1)
    away(1)
    for d in range(8):
        zero_slot(d)
    back(0)
    place(1)
    list_(0)
    ts(["AF"], ["W1"], T.W1[:], T.AF[:], 1.5, None, ALU.is_gt)
    swap(1)
    scatter(1)
    back(1)
    ts(["AF"], ["W2"], T.W2[:], T.AF[:], 3.5, None, ALU.is_lt)
    list_(1)
    for d in range(2, 8):
        scatter(d)
    ts(["AF"], ["V4"], T.V4[:], T.AF[:], 4.0, None, ALU.is_equal)
    ts(["AF"], ["V1"], T.V1[:], T.AF[:], 1.5, None, ALU.is_lt)
    tt(["W1", "W2"], ["W3"], T.W3[:], T.W1[:], T.W2[:], ALU.mult)
    ts(AX + ["IRf"], ["AX0"], T.AX0[:], T.IRf[:], 0.0, T.AX[:, 0:1], ALU.mult, ALU.add)
    for b in "012":
        fill("OF" + b, T["OF" + b][:], 1)
        fill("PS" + b, T["PS" + b][:, 0:96], 0.0)
    fill("TWs", T.TW[:, M:MW], 4194304.0)
    coefficients()
    for b in "012":
        ts(["IRf"], ["NX" + b], T["NX" + b][:], T.IRf[:, 0:32], 0.0, 1.0, ALU.mult, ALU.add)
    ts(["IRf", "KF"], ["IDf"], T.IDf[:], T.IRf[:], T.KF[:, 0:1], None, ALU.is_equal)

    def blocks(b):
        n = BATCH[b][1]
        return [(k, k * 128, min(n, k * 128 + 128)) for k in range(3)]

    def sources(lo, hi):
        return (["PL0"] if lo < 256 else []) + ["PL%d" % d for d in range(1, 8) if lo < 256 + 96 * d and hi > 160 + 96 * d]

    def visit(b, t):
        lo, n = BATCH[b]
        offs = T["OF%d" % b][:, 0:n // 16]
        out, pt = T["D1_%d" % b][:, 0:n], T.PL[:, lo:lo + n]
        rs, ws = TW + sources(lo, lo + n), ["D1_%d" % b]
        if t == 1:
            ts(rs, ws, out, pt, T.TW[:, 1:2], None, ALU.is_lt)
        else:
            tt(rs + ["OF%d" % b], ws, out, T.TW[:].indirect(offs), pt, ALU.is_gt)
        act(AX + ["OF%d" % b], ["D2_%d" % b], T["D2_%d" % b][:, 0:n], T.AX[:].indirect(offs), COPY)
        for (j, x, y) in blocks(b):
            out = T["PS%d" % b][0:y - x, j * 32:j * 32 + 32]
            mm(["D2_%d" % b, "C2"], ["PS%d" % b], out, T["D2_%d" % b][:, x:y], T.C2[:], True, False)
            mm(["D1_%d" % b, "C1"], ["PS%d" % b], out, T["D1_%d" % b][:, x:y], T.C1[:], False, True)

    def weigh(b):
        act(["PS%d" % b], ["ZZ%d" % b], T.ZZ[:, b * 48:b * 48 + 48], T["PS%d" % b][:, 1:96:2], RELU)

    def add_up(b, t):
        if b == 1:
            mm(["ZZ0", "ZZ1", "IDf"], ["AC"], T.AC[:, 0:96], T.IDf[:], T.ZZ[:, 0:96], t == 0, t == STEPS - 1)
        if b == 2:
            mm(["ZZ2", "IDf"], ["PF"], T.PF[:, 0:48], T.IDf[:], T.ZZ[:, 96:144], t == 0, t == STEPS - 1)

    def list_work(s):
        if s == 0:
            for k in (0, 1):
                ts([POS[k]], ["Q1_%d" % k], cols("Q1", k), T[POS[k]][:, 0:64], -96.0, None, ALU.add)
            ts(["CJ"], ["JT"], T.JT[:], T.CJ[:, 0:16], -1.0, -1.0, ALU.mult, ALU.add)
            fill("F0z", T.F0[:, 0:1152], 0.0)
        if s == 1:
            tt(["Q1_0", "Q1_1", "HB0", "HB1"], ["GQ"], T.GQ[:, 16:128], T.Q1[:, 16:128], T.HB[:, 16:128], ALU.mult)
            op("V", v.tensor_tensor, ["JT", "HB0"], ["GQ"], T.GQ[:, 0:16], T.JT[:], T.HB[:, 0:16], ALU.mult, add=True)
            vc(["F0z"], ["HITz"], T.HIT[:], T.F0[:, 0:1152])
        if s == 2:
            turn("GQ", "GX", T.GX[:], T.GQ[:])
            exchange(("GX", "GX"), "PR", 0, 4)
            vc(["F0z"], ["LOTz"], T.LOT[:], T.F0[:, 0:1152])
        if s == 4:
            turn("PR", "GT", T.GT[:], T.PR[:, 0:128])
        if s == 5:
            ts(["GT"], ["GO0"], T.GO[:, 0:16], T.GT[:, 0:16], 256.0, None, ALU.add)
            ts(["GT"], ["GO1"], T.GO[:, 16:128], T.GT[:, 16:128], 96.0, None, ALU.add)
            ts(["IRf", "KF"], ["IDh"], T.IDh[:], T.IRf[:], T.KF[:, 0:1], None, ALU.is_equal)

    for b in range(3):
        for (j, x, y) in blocks(b):
            mm(["AX0", "C2"], ["PS%d" % b], T["PS%d" % b][0:y - x, j * 32:j * 32 + 32], T.AX0[:, 0:y - x], T.C2[:], True, True)
        weigh(b)
        add_up(b, 0)
    for s in range(3 * STEPS):
        t, b = s // 3 + 1, s % 3
        t1, b1 = (s - 1) // 3 + 1, (s - 1) % 3
        t2, b2 = (s - 2) // 3 + 1, (s - 2) % 3
        go1, go2 = s >= 1 and t1 < STEPS, s >= 2 and t2 < STEPS
        visit(b, t)
        ps, nx, tmp, xt = "PS%d" % b1, "NX%d" % b1, "TT%d" % b1, "XT%d" % b1
        if go1:
            tt([ps, nx], [tmp], T[tmp][:], T[ps][:, 0:96:4], T[nx][:, 0:24], ALU.add)
        if go2:
            turn("EX", "WT%d" % b2, T["WT%d" % b2][:], T.EX[:, 0:32])
        if go1:
            tt([ps, tmp], [nx], T[nx][:, 0:24], T[ps][:, 2:96:4], T[tmp][:], ALU.min)
        if go2:
            vc(["WT%d" % b2], ["OF%d" % b2], T["OF%d" % b2][:], T["WT%d" % b2][:])
            weigh(b2)
        if go1:
            turn(nx, xt, T[xt][:], T[nx][:])
            exchange((xt, xt), "EX", 0, 1)
        if go2:
            add_up(b2, t2)
        if s >= 1 and t1 == STEPS:
            weigh(b1)
        list_work(s)
    weigh(2)

    def last_1(b):
        x = slice(b * 48, b * 48 + 48)
        acc = T.AC[:, x] if b < 2 else T.PF[:, 0:48]
        tt(["AC" if b < 2 else "PF", "ZZ%d" % b], ["EE%d" % b], T.EE[:, x], acc, T.ZZ[:, x], ALU.add)

    def last_2(b):
        tt(["EE%d" % b], ["SS%d" % b], T.SS[:, b * 24:b * 24 + 24], T.EE[:, b * 48:b * 48 + 48:2],
           T.EE[:, b * 48 + 1:b * 48 + 48:2], ALU.subtract)

    def last_3(b):
        vc(["SS%d" % b, "HITz"], ["HIT%d" % b], T.HIT[:, b * 384:b * 384 + 384:16], T.SS[:, b * 24:b * 24 + 24])

    def last_4(b):
        tt(["SS%d" % b, "HIT%d" % b, "LOTz"], ["LOT%d" % b], T.LOT[:, b * 384:b * 384 + 384:16],
           T.SS[:, b * 24:b * 24 + 24], T.HIT[:, b * 384:b * 384 + 384:16], ALU.subtract)

    def rows(b):
        ps = "PS%d" % b
        for (j, x, y) in blocks(b):
            c = (b * 3 + j) * 128
            mm(["HIT%d" % b, "IDh"], [ps], T[ps][:, x:y], T.HIT[:, c:c + 128], T.IDh[:, 0:y - x], True, False)
            mm(["LOT%d" % b, "IDh"], [ps], T[ps][:, x:y], T.LOT[:, c:c + 128], T.IDh[:, 0:y - x], False, True)
        if b == 0:
            act([ps], ["SA0"], T.SA[:, 0:64], T[ps][:, 256:320], COPY, scale=64.0)
            act([ps], ["RV0"], T.RW0[:, 0:256], T[ps][:, 0:256], COPY, scale=64.0)
        else:
            lo, n = BATCH[b][0] - 256, BATCH[b][1]
            act([ps], ["SA%d" % b], T.SA[:, lo:lo + n], T[ps][:, 0:n], COPY, scale=64.0)

    def send(ds, tags, cuts):
        deps("G", tags, [])
        trs = []
        for i, d in enumerate(ds):
            dst = cores[(rank - d) % N]
            rid, pid, _ = topo.addr(dst)
            es = topo.engines(core, dst)[cuts[i]:cuts[i + 1]]
            trs.append(RemoteDMATransfer(
                dst_ids=[DstId(rid=rid, pnc=pid)], dma_engine_mask=sum(1 << e for e in es), remote_sem=T.sem["rt%d" % d],
                srcs=[T.SA[:, 96 * (d - 1):96 * d]], dsts=[T["RW%d" % d][:, 0:96]]))
            total["ls"] += len(es)
            total["rt%d" % d] = len(topo.engines(cores[(rank + d) % N], core)[cuts[i]:cuts[i + 1]])
            note((None, "rt%d" % d, total["rt%d" % d]), [], ["RV%d" % d])
        g.remote_dma_fused(trs, local_sem=T.sem.ls)

    for f in (last_1, last_2, last_3, last_4):
        f(0)
        f(1)
    rows(0)
    rows(1)
    for f in (last_1, last_2, last_3, last_4):
        f(2)
    rows(2)
    send((1, 2, 3, 4), ["SA0", "SA1"], (0, 4, 8, 12, 16))
    send((5, 6, 7), ["SA2"], (0, 4, 8, 16))

    def sums_of(d):
        return T["RW%d" % d][:].indirect(T.GO[:, d * 16:d * 16 + 16]), ["RV%d" % d, "RZ%d" % d, "GO%d" % min(d, 1)]

    def plus(d, x, y):
        win, rs = sums_of(d)
        tt(rs + [x], [y], T[y][:], win, T[x][:], ALU.add)

    for d in range(3):
        win, rs = sums_of(d)
        act(rs, ["A%d" % d], T["A%d" % d][:], win, COPY)
    plus(3, "A0", "Y0")
    plus(4, "A1", "Y1")
    tt(["Y0", "A2"], ["Y2"], T.Y2[:], T.Y0[:], T.A2[:], ALU.add)
    tt(["Y1", "Y2"], ["Y3"], T.Y3[:], T.Y1[:], T.Y2[:], ALU.add)
    plus(5, "Y3", "Y0")
    plus(6, "Y0", "Y1")
    plus(7, "Y1", "Y2")
    dma("S", "dY", T.y[:, :], T.Y2[0::16, :], ["Y2"], ["y"])
    for sem in sorted(total):
        if max([seen.get((q, sem), 0) for q in queue]) < total[sem]:
            g.wait_ge(T.sem[sem], total[sem])
